import numpy as np
import ml_dtypes


def mxq(x, axis, fmt="e4m3"):
    dtype, down = {"e4m3": (ml_dtypes.float8_e4m3fn, 7), "e5m2": (ml_dtypes.float8_e5m2, 14)}[fmt]
    v = np.moveaxis(np.asarray(x, np.float32).astype(ml_dtypes.bfloat16).astype(np.float64), axis, -1)
    blocks = v.reshape(v.shape[:-1] + (-1, 32))
    amax = np.abs(blocks).max(-1, keepdims=True)
    byte = np.maximum(np.where(amax > 0, np.frexp(amax)[1] - 1 + 127, 0) - down, 1)
    scale = np.exp2(byte - 127.0)
    codes = (blocks / scale).astype(np.float32).astype(dtype).astype(np.float64)
    return np.moveaxis((codes * scale).reshape(v.shape), -1, axis)


WIDE = False


def mx_kscale(k):
    if not WIDE:
        return np.ones(k)
    levels = np.array([10, -10, 5, -5, 0])
    if k % 512:
        return np.exp2(np.random.permutation(np.resize(levels, k // 32))).repeat(32)
    a = np.empty((k // 512, 16))
    for p in range(k // 512):
        a[p, :8] = np.random.permutation(np.resize(levels, 8))
        for g in range(8):
            far = levels[np.abs(levels - a[p, g]) >= 10]
            a[p, g + 8] = far[np.random.randint(len(far))]
    return np.exp2(a.ravel()).repeat(32)


def f64(x):
    return np.asarray(x).astype(np.float64)


def striped(idx):
    return np.tile(idx.reshape(-1, 16).T, (8, 1)).astype(np.uint16)


def unstriped(offs):
    return offs[:16].T.reshape(-1).astype(np.int64)


K, T, D, S, V, N = 512, 4096, 3, 1536, 512, 128


def setup_inputs():
    n = np.random.standard_normal
    s = mx_kscale(K)[:, None]
    return {
        "xT": (n((K, T)) * s / np.sqrt(D)).astype(ml_dtypes.bfloat16).astype(np.float32),
        "w": (n((K, N)) / np.sqrt(K) / s).astype(np.float32),
        "b": (0.3 * n((N, 1))).astype(np.float32),
        "offs": striped(np.concatenate([np.random.permutation(T)[:V] for _ in range(D)])),
    }


def reference(xT, w, b, offs):
    idx = unstriped(offs)
    x = sum(f64(xT)[:, idx[d * V:(d + 1) * V]] for d in range(D))
    return (mxq(f64(w), 0, "e4m3").T @ mxq(x, 0, "e4m3")) + f64(b)

@@ -1,0 +1,122 @@
+from contextlib import ExitStack
+
+import concourse.mybir as mybir
+from concourse.masks import make_identity
+
+K, T, D, V, N = 512, 4096, 3, 512, 128
+S = D * V
+FLOPS = 2 * K * V * N
+
+F32 = mybir.dt.float32
+BF16 = mybir.dt.bfloat16
+U32 = mybir.dt.uint32
+U16 = mybir.dt.uint16
+U8 = mybir.dt.uint8
+FP8X4 = mybir.dt.float8_e4m3fn_x4
+ACT = mybir.ActivationFunctionType
+ADD = mybir.AluOpType.add
+
+P = 128
+PACK = 4
+PER_COL = 16
+CHUNKS = ((0, 256), (256, 512))
+
+
+def tile_picked_hash_lin_bias_sub_l_kernel(tc, xT, w, b, offs, out):
+    nc = tc.nc
+    with ExitStack() as ctx:
+        keep = ctx.enter_context(tc.tile_pool(name="keep", bufs=1))
+        ring = ctx.enter_context(tc.tile_pool(name="ring", bufs=2))
+        psum = ctx.enter_context(tc.psum_pool(name="psum", bufs=2))
+
+        offsets = keep.tile([P, S // PER_COL], U16, name="offsets")
+        planes = [keep.tile([P, T], F32, name=f"plane{t}") for t in range(PACK)]
+        picked = [keep.tile([P, S], F32, name=f"picked{t}") for t in range(PACK)]
+        w_raw = keep.tile([P, PACK, N], F32, name="w_raw")
+        bias = keep.tile([P, 1], F32, name="bias")
+        x_rows = xT.rearrange("(p t) c -> p t c", t=PACK)
+
+        nc.sync.dma_start(planes[0][:], x_rows[:, 0, :])
+        nc.sync.dma_start(offsets[:], offs)
+        for t in range(1, PACK):
+            nc.sync.dma_start(planes[t][:], x_rows[:, t, :])
+        nc.sync.dma_start(w_raw[:], w.rearrange("(p t) m -> p t m", t=PACK))
+        nc.sync.dma_start(bias[:], b)
+
+        ident_f32 = keep.tile([P, P], F32, name="ident_f32")
+        ident_bf16 = keep.tile([P, P], BF16, name="ident_bf16")
+        make_identity(nc, ident_f32[:])
+        make_identity(nc, ident_bf16[:])
+
+        x_grouped = keep.tile([P, V, PACK], BF16, name="x_grouped", align_bytes=64)
+        x_codes = keep.tile([P, V], U32, name="x_codes", align_bytes=64)
+        x_scales = keep.tile([P, V], U8, name="x_scales", align_bytes=64)
+        w_grouped = keep.tile([P, N, PACK], BF16, name="w_grouped", align_bytes=64)
+        w_codes = keep.tile([P, N], U32, name="w_codes", align_bytes=64)
+        w_scales = keep.tile([P, N], U8, name="w_scales", align_bytes=64)
+        result = keep.tile([P, V], F32, name="result")
+
+        def gather(t):
+            for d in range(D):
+                piece = offsets[:, d * V // PER_COL : (d + 1) * V // PER_COL]
+                nc.vector.tensor_copy(picked[t][:, d * V : (d + 1) * V], planes[t][:].indirect(piece))
+
+        def sum_on_tensor_engine(t):
+            turned = psum.tile([P, V], F32, name="turned")
+            for v0 in range(0, V, P):
+                for d in range(D):
+                    nc.tensor.matmul(
+                        turned[:, v0 : v0 + P],
+                        picked[t][:, d * V + v0 : d * V + v0 + P],
+                        ident_f32[:],
+                        start=(d == 0),
+                        stop=(d == D - 1),
+                        is_transpose=True,
+                    )
+            rounded = ring.tile([P, V], BF16, name="rounded")
+            nc.scalar.activation(rounded[:], turned[:], ACT.Copy)
+            back = psum.tile([P, V], BF16, name="back")
+            for v0 in range(0, V, P):
+                nc.tensor.transpose(back[:, v0 : v0 + P], rounded[:, v0 : v0 + P], ident_bf16[:])
+            if t < PACK - 2:
+                nc.scalar.copy(x_grouped[:, :, t], back[:])
+            else:
+                nc.scalar.copy(x_grouped[:, :, t : t + 2], back[:].unsqueeze(2).to_broadcast([P, V, 2]))
+
+        for t in range(PACK - 1):
+            gather(t)
+            sum_on_tensor_engine(t)
+        last = PACK - 1
+        gather(last)
+
+        nc.scalar.copy(w_grouped[:], w_raw[:].rearrange("p t m -> p m t"))
+        nc.vector.quantize_mx(
+            out=w_codes[:].bitcast(FP8X4), scales=w_scales[:], in_=w_grouped[:].rearrange("p m t -> p (m t)")
+        )
+
+        by_piece = picked[last][:].rearrange("p (d v) -> p v d", d=D)
+        for v0, v1 in CHUNKS:
+            with nc.allow_low_precision(reason="the sum is float32 inside the engine and rounded once"):
+                nc.vector.tensor_reduce(x_grouped[:, v0:v1, last], by_piece[:, v0:v1, :], mybir.AxisListType.X, ADD)
+        for v0, v1 in CHUNKS:
+            nc.vector.quantize_mx(
+                out=x_codes[:, v0:v1].bitcast(FP8X4),
+                scales=x_scales[:, v0:v1],
+                in_=x_grouped[:, v0:v1, :].rearrange("p v t -> p (v t)"),
+            )
+        for v0, v1 in CHUNKS:
+            acc = psum.tile([P, v1 - v0], F32, name="acc")
+            nc.tensor.matmul_mx(
+                out=acc[:],
+                lhsT=w_codes[:].bitcast(FP8X4),
+                lhsT_scale=w_scales[:],
+                rhs=x_codes[:, v0:v1].bitcast(FP8X4),
+                rhs_scale=x_scales[:, v0:v1],
+                start=True,
+                stop=True,
+            )
+            if v1 < V:
+                nc.scalar.activation(result[:, v0:v1], acc[:], ACT.Identity, bias=bias[:])
+            else:
+                nc.vector.tensor_scalar(result[:, v0:v1], acc[:], bias[:], None, ADD)
+            nc.sync.dma_start(out[:, v0:v1], result[:, v0:v1])

@@ -15,11 +15,14 @@ U8 = mybir.dt.uint8
 FP8X4 = mybir.dt.float8_e4m3fn_x4
 ACT = mybir.ActivationFunctionType
 ADD = mybir.AluOpType.add
+MULT = mybir.AluOpType.mult
 
 P = 128
 PACK = 4
 PER_COL = 16
-CHUNKS = ((0, 256), (256, 512))
+ORDER = (2, 0, 1, 3)
+HALF = V // 2
+CHUNKS = ((0, 256), (256, 384), (384, 512))
 
 
 def tile_picked_hash_lin_bias_sub_l_kernel(tc, xT, w, b, offs, out):
@@ -36,9 +39,9 @@ def tile_picked_hash_lin_bias_sub_l_kernel(tc, xT, w, b, offs, out):
         bias = keep.tile([P, 1], F32, name="bias")
         x_rows = xT.rearrange("(p t) c -> p t c", t=PACK)
 
-        nc.sync.dma_start(planes[0][:], x_rows[:, 0, :])
+        nc.sync.dma_start(planes[ORDER[0]][:], x_rows[:, ORDER[0], :])
         nc.sync.dma_start(offsets[:], offs)
-        for t in range(1, PACK):
+        for t in ORDER[1:]:
             nc.sync.dma_start(planes[t][:], x_rows[:, t, :])
         nc.sync.dma_start(w_raw[:], w.rearrange("(p t) m -> p t m", t=PACK))
         nc.sync.dma_start(bias[:], b)
@@ -48,6 +51,8 @@ def tile_picked_hash_lin_bias_sub_l_kernel(tc, xT, w, b, offs, out):
         make_identity(nc, ident_f32[:])
         make_identity(nc, ident_bf16[:])
 
+        ones = keep.tile([P, HALF], F32, name="ones")
+        nc.gpsimd.memset(ones[:], 1.0)
         x_grouped = keep.tile([P, V, PACK], BF16, name="x_grouped", align_bytes=64)
         x_codes = keep.tile([P, V], U32, name="x_codes", align_bytes=64)
         x_scales = keep.tile([P, V], U8, name="x_scales", align_bytes=64)
@@ -61,51 +66,68 @@ def tile_picked_hash_lin_bias_sub_l_kernel(tc, xT, w, b, offs, out):
                 piece = offsets[:, d * V // PER_COL : (d + 1) * V // PER_COL]
                 nc.vector.tensor_copy(picked[t][:, d * V : (d + 1) * V], planes[t][:].indirect(piece))
 
-        def sum_on_tensor_engine(t):
-            turned = psum.tile([P, V], F32, name="turned")
-            for v0 in range(0, V, P):
-                for d in range(D):
+        def sum_on_tensor_engine(t, blocks, blocks_a_bank):
+            turned = [psum.tile([P, P], F32, name="turned", bufs=4) for v0 in blocks]
+            for d in range(D):
+                for bank, v0 in zip(turned, blocks):
                     nc.tensor.matmul(
-                        turned[:, v0 : v0 + P],
+                        bank[:],
                         picked[t][:, d * V + v0 : d * V + v0 + P],
                         ident_f32[:],
                         start=(d == 0),
                         stop=(d == D - 1),
                         is_transpose=True,
                     )
-            rounded = ring.tile([P, V], BF16, name="rounded")
-            nc.scalar.activation(rounded[:], turned[:], ACT.Copy)
-            back = psum.tile([P, V], BF16, name="back")
-            for v0 in range(0, V, P):
-                nc.tensor.transpose(back[:, v0 : v0 + P], rounded[:, v0 : v0 + P], ident_bf16[:])
-            if t < PACK - 2:
-                nc.scalar.copy(x_grouped[:, :, t], back[:])
-            else:
-                nc.scalar.copy(x_grouped[:, :, t : t + 2], back[:].unsqueeze(2).to_broadcast([P, V, 2]))
+            rounded = ring.tile([P, len(blocks), P], BF16, name="rounded")
+            for j, bank in enumerate(turned):
+                nc.scalar.activation(rounded[:, j, :], bank[:], ACT.Copy)
+            for j0 in range(0, len(blocks), blocks_a_bank):
+                width = blocks_a_bank * P
+                back = psum.tile([P, width], BF16, name="back")
+                for j in range(blocks_a_bank):
+                    nc.tensor.transpose(back[:, j * P : (j + 1) * P], rounded[:, j0 + j, :], ident_bf16[:])
+                cols = slice(blocks[j0], blocks[j0] + width)
+                if t + 1 == last:
+                    nc.scalar.copy(x_grouped[:, cols, t : t + 2], back[:].unsqueeze(2).to_broadcast([P, width, 2]))
+                else:
+                    nc.scalar.copy(x_grouped[:, cols, t], back[:])
 
-        for t in range(PACK - 1):
-            gather(t)
-            sum_on_tensor_engine(t)
-        last = PACK - 1
-        gather(last)
-
-        nc.scalar.copy(w_grouped[:], w_raw[:].rearrange("p t m -> p m t"))
-        nc.vector.quantize_mx(
-            out=w_codes[:].bitcast(FP8X4), scales=w_scales[:], in_=w_grouped[:].rearrange("p m t -> p (m t)")
-        )
-
-        by_piece = picked[last][:].rearrange("p (d v) -> p v d", d=D)
-        for v0, v1 in CHUNKS:
-            with nc.allow_low_precision(reason="the sum is float32 inside the engine and rounded once"):
-                nc.vector.tensor_reduce(x_grouped[:, v0:v1, last], by_piece[:, v0:v1, :], mybir.AxisListType.X, ADD)
-        for v0, v1 in CHUNKS:
+        def quantize_x(v0, v1):
             nc.vector.quantize_mx(
                 out=x_codes[:, v0:v1].bitcast(FP8X4),
                 scales=x_scales[:, v0:v1],
                 in_=x_grouped[:, v0:v1, :].rearrange("p v t -> p (v t)"),
             )
+
+        last = ORDER[-1]
+        for t in ORDER[:-1]:
+            gather(t)
+            sum_on_tensor_engine(t, list(range(0, V, P)), V // P)
+
+        nc.scalar.copy(w_grouped[:], w_raw[:].rearrange("p t m -> p m t"))
+
+        for v0 in (0, HALF):
+            for d in range(D):
+                j0 = d * V + v0
+                piece = offsets[:, j0 // PER_COL : (j0 + HALF) // PER_COL]
+                nc.vector.tensor_tensor(picked[last][:, j0 : j0 + HALF], planes[last][:].indirect(piece), ones[:], MULT)
+        sum_on_tensor_engine(last, list(range(0, HALF, P)), 1)
+
+        partial = keep.tile([P, V], F32, name="partial")
+        summed = keep.tile([P, V], BF16, name="summed")
+        for v0, v1 in CHUNKS[1:]:
+            nc.vector.tensor_tensor(partial[:, v0:v1], picked[last][:, v0:v1], picked[last][:, V + v0 : V + v1], ADD)
+        for v0, v1 in CHUNKS[1:]:
+            nc.vector.tensor_tensor(summed[:, v0:v1], partial[:, v0:v1], picked[last][:, 2 * V + v0 : 2 * V + v1], ADD)
+        for v0, v1 in CHUNKS[1:]:
+            nc.vector.tensor_copy(x_grouped[:, v0:v1, last], summed[:, v0:v1])
+        nc.vector.quantize_mx(
+            out=w_codes[:].bitcast(FP8X4), scales=w_scales[:], in_=w_grouped[:].rearrange("p m t -> p (m t)")
+        )
         for v0, v1 in CHUNKS:
-            acc = psum.tile([P, v1 - v0], F32, name="acc")
+            quantize_x(v0, v1)
+        for v0, v1 in CHUNKS:
+            acc = psum.tile([P, v1 - v0], F32, name="acc", tag="turned", bufs=4)
             nc.tensor.matmul_mx(
                 out=acc[:],
                 lhsT=w_codes[:].bitcast(FP8X4),

@@ -22,7 +22,7 @@ PACK = 4
 PER_COL = 16
 ORDER = (2, 0, 1, 3)
 HALF = V // 2
-CHUNKS = ((0, 256), (256, 384), (384, 512))
+CHUNKS = ((0, 256), (256, 512))
 
 
 def tile_picked_hash_lin_bias_sub_l_kernel(tc, xT, w, b, offs, out):
@@ -61,10 +61,11 @@ def tile_picked_hash_lin_bias_sub_l_kernel(tc, xT, w, b, offs, out):
         w_scales = keep.tile([P, N], U8, name="w_scales", align_bytes=64)
         result = keep.tile([P, V], F32, name="result")
 
-        def gather(t):
+        def gather(t, v0, v1):
             for d in range(D):
-                piece = offsets[:, d * V // PER_COL : (d + 1) * V // PER_COL]
-                nc.vector.tensor_copy(picked[t][:, d * V : (d + 1) * V], planes[t][:].indirect(piece))
+                j0, j1 = d * V + v0, d * V + v1
+                piece = offsets[:, j0 // PER_COL : j1 // PER_COL]
+                nc.vector.tensor_tensor(picked[t][:, j0:j1], planes[t][:].indirect(piece), ones[:, : v1 - v0], MULT)
 
         def sum_on_tensor_engine(t, blocks, blocks_a_bank):
             turned = [psum.tile([P, P], F32, name="turned", bufs=4) for v0 in blocks]
@@ -83,7 +84,7 @@ def tile_picked_hash_lin_bias_sub_l_kernel(tc, xT, w, b, offs, out):
                 nc.scalar.activation(rounded[:, j, :], bank[:], ACT.Copy)
             for j0 in range(0, len(blocks), blocks_a_bank):
                 width = blocks_a_bank * P
-                back = psum.tile([P, width], BF16, name="back")
+                back = psum.tile([P, width], BF16, name="back", bufs=3)
                 for j in range(blocks_a_bank):
                     nc.tensor.transpose(back[:, j * P : (j + 1) * P], rounded[:, j0 + j, :], ident_bf16[:])
                 cols = slice(blocks[j0], blocks[j0] + width)
@@ -101,31 +102,27 @@ def tile_picked_hash_lin_bias_sub_l_kernel(tc, xT, w, b, offs, out):
 
         last = ORDER[-1]
         for t in ORDER[:-1]:
-            gather(t)
-            sum_on_tensor_engine(t, list(range(0, V, P)), V // P)
+            for v0, v1 in CHUNKS:
+                gather(t, v0, v1)
+                sum_on_tensor_engine(t, list(range(v0, v1, P)), 2)
 
         nc.scalar.copy(w_grouped[:], w_raw[:].rearrange("p t m -> p m t"))
 
-        for v0 in (0, HALF):
-            for d in range(D):
-                j0 = d * V + v0
-                piece = offsets[:, j0 // PER_COL : (j0 + HALF) // PER_COL]
-                nc.vector.tensor_tensor(picked[last][:, j0 : j0 + HALF], planes[last][:].indirect(piece), ones[:], MULT)
-        sum_on_tensor_engine(last, list(range(0, HALF, P)), 1)
-
-        partial = keep.tile([P, V], F32, name="partial")
-        summed = keep.tile([P, V], BF16, name="summed")
-        for v0, v1 in CHUNKS[1:]:
-            nc.vector.tensor_tensor(partial[:, v0:v1], picked[last][:, v0:v1], picked[last][:, V + v0 : V + v1], ADD)
-        for v0, v1 in CHUNKS[1:]:
-            nc.vector.tensor_tensor(summed[:, v0:v1], partial[:, v0:v1], picked[last][:, 2 * V + v0 : 2 * V + v1], ADD)
-        for v0, v1 in CHUNKS[1:]:
-            nc.vector.tensor_copy(x_grouped[:, v0:v1, last], summed[:, v0:v1])
+        for v0, v1 in ((0, HALF), (HALF, V - P)):
+            gather(last, v0, v1)
+            sum_on_tensor_engine(last, list(range(v0, v1, P)), 1)
+        gather(last, V - P, V)
+        partial = keep.tile([P, P], F32, name="partial")
+        summed = keep.tile([P, P], BF16, name="summed")
+        nc.vector.tensor_tensor(partial[:], picked[last][:, V - P : V], picked[last][:, 2 * V - P : 2 * V], ADD)
         nc.vector.quantize_mx(
             out=w_codes[:].bitcast(FP8X4), scales=w_scales[:], in_=w_grouped[:].rearrange("p m t -> p (m t)")
         )
-        for v0, v1 in CHUNKS:
-            quantize_x(v0, v1)
+        nc.vector.tensor_tensor(summed[:], partial[:], picked[last][:, 3 * V - P : 3 * V], ADD)
+        quantize_x(0, P)
+        nc.vector.tensor_copy(x_grouped[:, V - P : V, last], summed[:])
+        quantize_x(P, HALF)
+        quantize_x(HALF, V)
         for v0, v1 in CHUNKS:
             acc = psum.tile([P, v1 - v0], F32, name="acc", tag="turned", bufs=4)
             nc.tensor.matmul_mx(

@@ -1,7 +1,6 @@
 from contextlib import ExitStack
 
 import concourse.mybir as mybir
-from concourse.masks import make_identity
 
 K, T, D, V, N = 512, 4096, 3, 512, 128
 S = D * V
@@ -20,111 +19,61 @@ MULT = mybir.AluOpType.mult
 P = 128
 PACK = 4
 PER_COL = 16
-ORDER = (2, 0, 1, 3)
 HALF = V // 2
-CHUNKS = ((0, 256), (256, 512))
 
 
 def tile_picked_hash_lin_bias_sub_l_kernel(tc, xT, w, b, offs, out):
     nc = tc.nc
     with ExitStack() as ctx:
         keep = ctx.enter_context(tc.tile_pool(name="keep", bufs=1))
-        ring = ctx.enter_context(tc.tile_pool(name="ring", bufs=2))
-        psum = ctx.enter_context(tc.psum_pool(name="psum", bufs=2))
+        psum = ctx.enter_context(tc.psum_pool(name="psum", bufs=1))
 
         offsets = keep.tile([P, S // PER_COL], U16, name="offsets")
         planes = [keep.tile([P, T], F32, name=f"plane{t}") for t in range(PACK)]
-        picked = [keep.tile([P, S], F32, name=f"picked{t}") for t in range(PACK)]
         w_raw = keep.tile([P, PACK, N], F32, name="w_raw")
         bias = keep.tile([P, 1], F32, name="bias")
         x_rows = xT.rearrange("(p t) c -> p t c", t=PACK)
 
-        nc.sync.dma_start(planes[ORDER[0]][:], x_rows[:, ORDER[0], :])
+        nc.sync.dma_start(planes[0][:], x_rows[:, 0, :])
         nc.sync.dma_start(offsets[:], offs)
-        for t in ORDER[1:]:
+        for t in range(1, PACK):
             nc.sync.dma_start(planes[t][:], x_rows[:, t, :])
         nc.sync.dma_start(w_raw[:], w.rearrange("(p t) m -> p t m", t=PACK))
         nc.sync.dma_start(bias[:], b)
 
-        ident_f32 = keep.tile([P, P], F32, name="ident_f32")
-        ident_bf16 = keep.tile([P, P], BF16, name="ident_bf16")
-        make_identity(nc, ident_f32[:])
-        make_identity(nc, ident_bf16[:])
-
         ones = keep.tile([P, HALF], F32, name="ones")
         nc.gpsimd.memset(ones[:], 1.0)
         x_grouped = keep.tile([P, V, PACK], BF16, name="x_grouped", align_bytes=64)
-        x_codes = keep.tile([P, V], U32, name="x_codes", align_bytes=64)
         x_scales = keep.tile([P, V], U8, name="x_scales", align_bytes=64)
         w_grouped = keep.tile([P, N, PACK], BF16, name="w_grouped", align_bytes=64)
-        w_codes = keep.tile([P, N], U32, name="w_codes", align_bytes=64)
         w_scales = keep.tile([P, N], U8, name="w_scales", align_bytes=64)
         result = keep.tile([P, V], F32, name="result")
 
-        def gather(t, v0, v1):
-            for d in range(D):
-                j0, j1 = d * V + v0, d * V + v1
-                piece = offsets[:, j0 // PER_COL : j1 // PER_COL]
-                nc.vector.tensor_tensor(picked[t][:, j0:j1], planes[t][:].indirect(piece), ones[:, : v1 - v0], MULT)
+        def gather(t, d, cols, before, tag):
+            v0, v1 = cols
+            piece = offsets[:, (d * V + v0) // PER_COL : (d * V + v1) // PER_COL]
+            looked_up = planes[t][:].indirect(piece)
+            total = keep.tile([P, v1 - v0], F32, name="total", tag=tag, align_bytes=64)
+            if before is not None:
+                nc.vector.tensor_tensor(total[:], looked_up, before, ADD)
+            elif v1 - v0 == V:
+                nc.vector.tensor_copy(total[:], looked_up)
+            else:
+                nc.vector.tensor_tensor(total[:], looked_up, ones[:, : v1 - v0], MULT)
+            return total
 
-        def sum_on_tensor_engine(t, blocks, blocks_a_bank):
-            turned = [psum.tile([P, P], F32, name="turned", bufs=4) for v0 in blocks]
-            for d in range(D):
-                for bank, v0 in zip(turned, blocks):
-                    nc.tensor.matmul(
-                        bank[:],
-                        picked[t][:, d * V + v0 : d * V + v0 + P],
-                        ident_f32[:],
-                        start=(d == 0),
-                        stop=(d == D - 1),
-                        is_transpose=True,
-                    )
-            rounded = ring.tile([P, len(blocks), P], BF16, name="rounded")
-            for j, bank in enumerate(turned):
-                nc.scalar.activation(rounded[:, j, :], bank[:], ACT.Copy)
-            for j0 in range(0, len(blocks), blocks_a_bank):
-                width = blocks_a_bank * P
-                back = psum.tile([P, width], BF16, name="back", bufs=3)
-                for j in range(blocks_a_bank):
-                    nc.tensor.transpose(back[:, j * P : (j + 1) * P], rounded[:, j0 + j, :], ident_bf16[:])
-                cols = slice(blocks[j0], blocks[j0] + width)
-                if t + 1 == last:
-                    nc.scalar.copy(x_grouped[:, cols, t : t + 2], back[:].unsqueeze(2).to_broadcast([P, width, 2]))
-                else:
-                    nc.scalar.copy(x_grouped[:, cols, t], back[:])
+        def interleave(t, cols, total):
+            nc.scalar.copy(x_grouped[:, cols[0] : cols[1], t], total[:])
 
-        def quantize_x(v0, v1):
+        def quantize_x(x_codes, v0, v1):
             nc.vector.quantize_mx(
                 out=x_codes[:, v0:v1].bitcast(FP8X4),
                 scales=x_scales[:, v0:v1],
                 in_=x_grouped[:, v0:v1, :].rearrange("p v t -> p (v t)"),
             )
 
-        last = ORDER[-1]
-        for t in ORDER[:-1]:
-            for v0, v1 in CHUNKS:
-                gather(t, v0, v1)
-                sum_on_tensor_engine(t, list(range(v0, v1, P)), 2)
-
-        nc.scalar.copy(w_grouped[:], w_raw[:].rearrange("p t m -> p m t"))
-
-        for v0, v1 in ((0, HALF), (HALF, V - P)):
-            gather(last, v0, v1)
-            sum_on_tensor_engine(last, list(range(v0, v1, P)), 1)
-        gather(last, V - P, V)
-        partial = keep.tile([P, P], F32, name="partial")
-        summed = keep.tile([P, P], BF16, name="summed")
-        nc.vector.tensor_tensor(partial[:], picked[last][:, V - P : V], picked[last][:, 2 * V - P : 2 * V], ADD)
-        nc.vector.quantize_mx(
-            out=w_codes[:].bitcast(FP8X4), scales=w_scales[:], in_=w_grouped[:].rearrange("p m t -> p (m t)")
-        )
-        nc.vector.tensor_tensor(summed[:], partial[:], picked[last][:, 3 * V - P : 3 * V], ADD)
-        quantize_x(0, P)
-        nc.vector.tensor_copy(x_grouped[:, V - P : V, last], summed[:])
-        quantize_x(P, HALF)
-        quantize_x(HALF, V)
-        for v0, v1 in CHUNKS:
-            acc = psum.tile([P, v1 - v0], F32, name="acc", tag="turned", bufs=4)
+        def product(x_codes, w_codes, v0, v1, on_scalar):
+            acc = psum.tile([P, v1 - v0], F32, name=f"acc{v0}")
             nc.tensor.matmul_mx(
                 out=acc[:],
                 lhsT=w_codes[:].bitcast(FP8X4),
@@ -134,8 +83,44 @@ def tile_picked_hash_lin_bias_sub_l_kernel(tc, xT, w, b, offs, out):
                 start=True,
                 stop=True,
             )
-            if v1 < V:
+            if on_scalar:
                 nc.scalar.activation(result[:, v0:v1], acc[:], ACT.Identity, bias=bias[:])
             else:
                 nc.vector.tensor_scalar(result[:, v0:v1], acc[:], bias[:], None, ADD)
-            nc.sync.dma_start(out[:, v0:v1], result[:, v0:v1])
+
+        last = PACK - 1
+        halves = ((0, HALF), (HALF, V))
+        for t in range(last):
+            one = gather(t, 0, (0, V), None, "early0")
+            two = [gather(t, 1, h, one[:, h[0] : h[1]], f"early1_{h[0]}") for h in halves]
+            three = [gather(t, 2, h, s[:], f"early2_{h[0]}") for h, s in zip(halves, two)]
+            for h, s in zip(halves, three):
+                interleave(t, h, s)
+
+        nc.scalar.copy(w_grouped[:], w_raw[:].rearrange("p t m -> p m t"))
+
+        first, third, fourth = (0, HALF), (HALF, HALF + P), (HALF + P, V)
+        x0 = gather(last, 0, first, None, "a")
+        y0 = gather(last, 0, third, None, "y0")
+        x1 = gather(last, 1, first, x0[:], "x1")
+        y1 = gather(last, 1, third, y0[:], "b")
+        x2 = gather(last, 2, first, x1[:], "x2")
+        interleave(last, first, x2)
+        z0 = gather(last, 0, fourth, None, "a")
+        y2 = gather(last, 2, third, y1[:], "y2")
+        interleave(last, third, y2)
+        z1 = gather(last, 1, fourth, z0[:], "z1")
+        w_codes = keep.tile([P, N], U32, name="w_codes", tag="b", align_bytes=64)
+        nc.vector.quantize_mx(
+            out=w_codes[:].bitcast(FP8X4), scales=w_scales[:], in_=w_grouped[:].rearrange("p m t -> p (m t)")
+        )
+        z2 = gather(last, 2, fourth, z1[:], "z2")
+        interleave(last, fourth, z2)
+        x_codes = keep.tile([P, V], U32, name="x_codes", tag="a", align_bytes=64)
+        for cols in (first, third, fourth):
+            quantize_x(x_codes, *cols)
+        product(x_codes, w_codes, *first, True)
+        nc.sync.dma_start(out[:, :HALF], result[:, :HALF])
+        product(x_codes, w_codes, *third, False)
+        product(x_codes, w_codes, *fourth, True)
+        nc.sync.dma_start(out[:, HALF:], result[:, HALF:])

@@ -20,6 +20,7 @@ P = 128
 PACK = 4
 PER_COL = 16
 HALF = V // 2
+TAIL = 64
 
 
 def tile_picked_hash_lin_bias_sub_l_kernel(tc, xT, w, b, offs, out):
@@ -42,28 +43,34 @@ def tile_picked_hash_lin_bias_sub_l_kernel(tc, xT, w, b, offs, out):
         nc.sync.dma_start(bias[:], b)
 
         ones = keep.tile([P, HALF], F32, name="ones")
-        nc.gpsimd.memset(ones[:], 1.0)
+        ones_y = keep.tile([P, P], F32, name="ones_y", tag="a", align_bytes=64)
+        ones_z = keep.tile([P, P], F32, name="ones_z", tag="b", align_bytes=64)
+        for filled in (ones, ones_y, ones_z):
+            nc.gpsimd.memset(filled[:], 1.0)
         x_grouped = keep.tile([P, V, PACK], BF16, name="x_grouped", align_bytes=64)
         x_scales = keep.tile([P, V], U8, name="x_scales", align_bytes=64)
         w_grouped = keep.tile([P, N, PACK], BF16, name="w_grouped", align_bytes=64)
         w_scales = keep.tile([P, N], U8, name="w_scales", align_bytes=64)
         result = keep.tile([P, V], F32, name="result")
 
-        def gather(t, d, cols, before, tag):
+        def gather(t, d, cols, before, tag, op=ADD):
             v0, v1 = cols
             piece = offsets[:, (d * V + v0) // PER_COL : (d * V + v1) // PER_COL]
             looked_up = planes[t][:].indirect(piece)
             total = keep.tile([P, v1 - v0], F32, name="total", tag=tag, align_bytes=64)
             if before is not None:
-                nc.vector.tensor_tensor(total[:], looked_up, before, ADD)
-            elif v1 - v0 == V:
-                nc.vector.tensor_copy(total[:], looked_up)
+                nc.vector.tensor_tensor(total[:], looked_up, before, op)
             else:
-                nc.vector.tensor_tensor(total[:], looked_up, ones[:, : v1 - v0], MULT)
+                nc.vector.tensor_copy(total[:], looked_up)
             return total
 
         def interleave(t, cols, total):
-            nc.scalar.copy(x_grouped[:, cols[0] : cols[1], t], total[:])
+            v0, v1 = cols
+            if t >= 2 and v1 == V:
+                nc.scalar.copy(x_grouped[:, v0 : V - TAIL, t], total[:, : V - TAIL - v0])
+                nc.vector.tensor_copy(x_grouped[:, V - TAIL : V, t], total[:, V - TAIL - v0 :])
+            else:
+                nc.scalar.copy(x_grouped[:, v0:v1, t], total[:])
 
         def quantize_x(x_codes, v0, v1):
             nc.vector.quantize_mx(
@@ -100,27 +107,26 @@ def tile_picked_hash_lin_bias_sub_l_kernel(tc, xT, w, b, offs, out):
         nc.scalar.copy(w_grouped[:], w_raw[:].rearrange("p t m -> p m t"))
 
         first, third, fourth = (0, HALF), (HALF, HALF + P), (HALF + P, V)
-        x0 = gather(last, 0, first, None, "a")
-        y0 = gather(last, 0, third, None, "y0")
+        x0 = gather(last, 0, first, ones[:], "x0", MULT)
+        y0 = gather(last, 0, third, ones_y[:], "y0", MULT)
         x1 = gather(last, 1, first, x0[:], "x1")
-        y1 = gather(last, 1, third, y0[:], "b")
+        z0 = gather(last, 0, fourth, ones_z[:], "a", MULT)
         x2 = gather(last, 2, first, x1[:], "x2")
         interleave(last, first, x2)
-        z0 = gather(last, 0, fourth, None, "a")
+        y1 = gather(last, 1, third, y0[:], "b")
+        z1 = gather(last, 1, fourth, z0[:], "z1")
         y2 = gather(last, 2, third, y1[:], "y2")
         interleave(last, third, y2)
-        z1 = gather(last, 1, fourth, z0[:], "z1")
-        w_codes = keep.tile([P, N], U32, name="w_codes", tag="b", align_bytes=64)
+        z2 = gather(last, 2, fourth, z1[:], "z2")
+        w_codes = keep.tile([P, N], U32, name="w_codes", align_bytes=64)
         nc.vector.quantize_mx(
             out=w_codes[:].bitcast(FP8X4), scales=w_scales[:], in_=w_grouped[:].rearrange("p m t -> p (m t)")
         )
-        z2 = gather(last, 2, fourth, z1[:], "z2")
+        x_codes = keep.tile([P, V], U32, name="x_codes", tag="b", align_bytes=64)
+        quantize_x(x_codes, *first)
         interleave(last, fourth, z2)
-        x_codes = keep.tile([P, V], U32, name="x_codes", tag="a", align_bytes=64)
-        for cols in (first, third, fourth):
-            quantize_x(x_codes, *cols)
-        product(x_codes, w_codes, *first, True)
-        nc.sync.dma_start(out[:, :HALF], result[:, :HALF])
-        product(x_codes, w_codes, *third, False)
-        product(x_codes, w_codes, *fourth, True)
-        nc.sync.dma_start(out[:, HALF:], result[:, HALF:])
+        quantize_x(x_codes, *third)
+        quantize_x(x_codes, *fourth)
+        for cols, on_scalar in ((first, True), (third, True), (fourth, False)):
+            product(x_codes, w_codes, *cols, on_scalar)
+            nc.sync.dma_start(out[:, cols[0] : cols[1]], result[:, cols[0] : cols[1]])

@@ -1,6 +1,7 @@
 from contextlib import ExitStack
 
 import concourse.mybir as mybir
+from concourse.masks import make_identity
 
 K, T, D, V, N = 512, 4096, 3, 512, 128
 S = D * V
@@ -21,6 +22,7 @@ PACK = 4
 PER_COL = 16
 HALF = V // 2
 TAIL = 64
+ORDER = (2, 0, 1, 3)
 
 
 def tile_picked_hash_lin_bias_sub_l_kernel(tc, xT, w, b, offs, out):
@@ -35,13 +37,15 @@ def tile_picked_hash_lin_bias_sub_l_kernel(tc, xT, w, b, offs, out):
         bias = keep.tile([P, 1], F32, name="bias")
         x_rows = xT.rearrange("(p t) c -> p t c", t=PACK)
 
-        nc.sync.dma_start(planes[0][:], x_rows[:, 0, :])
+        nc.sync.dma_start(planes[ORDER[0]][:], x_rows[:, ORDER[0], :])
         nc.sync.dma_start(offsets[:], offs)
-        for t in range(1, PACK):
+        for t in ORDER[1:]:
             nc.sync.dma_start(planes[t][:], x_rows[:, t, :])
         nc.sync.dma_start(w_raw[:], w.rearrange("(p t) m -> p t m", t=PACK))
         nc.sync.dma_start(bias[:], b)
 
+        ident = keep.tile([P, P], F32, name="ident")
+        make_identity(nc, ident[:])
         ones = keep.tile([P, HALF], F32, name="ones")
         ones_y = keep.tile([P, P], F32, name="ones_y", tag="a", align_bytes=64)
         ones_z = keep.tile([P, P], F32, name="ones_z", tag="b", align_bytes=64)
@@ -66,11 +70,35 @@ def tile_picked_hash_lin_bias_sub_l_kernel(tc, xT, w, b, offs, out):
 
         def interleave(t, cols, total):
             v0, v1 = cols
-            if t >= 2 and v1 == V:
+            if t == last and v1 == V:
                 nc.scalar.copy(x_grouped[:, v0 : V - TAIL, t], total[:, : V - TAIL - v0])
                 nc.vector.tensor_copy(x_grouped[:, V - TAIL : V, t], total[:, V - TAIL - v0 :])
             else:
                 nc.scalar.copy(x_grouped[:, v0:v1, t], total[:])
+
+        def sum_on_tensor_engine(t):
+            turned = [psum.tile([P, P], F32, name="turned", bufs=4) for v0 in range(0, V, P)]
+            for d in range(D):
+                picked = gather(t, d, (0, V), None, f"picked{d}")
+                for j, bank in enumerate(turned):
+                    nc.tensor.matmul(
+                        bank[:],
+                        picked[:, j * P : (j + 1) * P],
+                        ident[:],
+                        start=(d == 0),
+                        stop=(d == D - 1),
+                        is_transpose=True,
+                    )
+            staged = keep.tile([P, V], F32, name="staged")
+            for j, bank in enumerate(turned):
+                nc.scalar.copy(staged[:, j * P : (j + 1) * P], bank[:])
+            back = psum.tile([P, V], F32, name="back")
+            for j in range(0, V, P):
+                nc.tensor.transpose(back[:, j : j + P], staged[:, j : j + P], ident[:])
+            if t + 1 == last:
+                nc.scalar.copy(x_grouped[:, :, t : t + 2], back[:].unsqueeze(2).to_broadcast([P, V, 2]))
+            else:
+                nc.scalar.copy(x_grouped[:, :, t], back[:])
 
         def quantize_x(x_codes, v0, v1):
             nc.vector.quantize_mx(
@@ -97,7 +125,9 @@ def tile_picked_hash_lin_bias_sub_l_kernel(tc, xT, w, b, offs, out):
 
         last = PACK - 1
         halves = ((0, HALF), (HALF, V))
-        for t in range(last):
+        for t in ORDER[:2]:
+            sum_on_tensor_engine(t)
+        for t in ORDER[2:3]:
             one = gather(t, 0, (0, V), None, "early0")
             two = [gather(t, 1, h, one[:, h[0] : h[1]], f"early1_{h[0]}") for h in halves]
             three = [gather(t, 2, h, s[:], f"early2_{h[0]}") for h, s in zip(halves, two)]

@@ -31,9 +31,9 @@ def tile_picked_hash_lin_bias_sub_l_kernel(tc, xT, w, b, offs, out):
         keep = ctx.enter_context(tc.tile_pool(name="keep", bufs=1))
         psum = ctx.enter_context(tc.psum_pool(name="psum", bufs=1))
 
-        offsets = keep.tile([P, S // PER_COL], U16, name="offsets")
-        planes = [keep.tile([P, T], F32, name=f"plane{t}") for t in range(PACK)]
-        w_raw = keep.tile([P, PACK, N], F32, name="w_raw")
+        offsets = keep.tile([P, S // PER_COL], U16, name="offsets", align_bytes=256)
+        planes = [keep.tile([P, T], F32, name=f"plane{t}", align_bytes=256) for t in range(PACK)]
+        w_raw = keep.tile([P, PACK, N], F32, name="w_raw", align_bytes=256)
         bias = keep.tile([P, 1], F32, name="bias")
         x_rows = xT.rearrange("(p t) c -> p t c", t=PACK)
 
@@ -55,7 +55,7 @@ def tile_picked_hash_lin_bias_sub_l_kernel(tc, xT, w, b, offs, out):
         x_scales = keep.tile([P, V], U8, name="x_scales", align_bytes=64)
         w_grouped = keep.tile([P, N, PACK], BF16, name="w_grouped", align_bytes=64)
         w_scales = keep.tile([P, N], U8, name="w_scales", align_bytes=64)
-        result = keep.tile([P, V], F32, name="result")
+        result = keep.tile([P, V], F32, name="result", align_bytes=256)
 
         def gather(t, d, cols, before, tag, op=ADD):
             v0, v1 = cols

@@ -1,7 +1,6 @@
 from contextlib import ExitStack
 
 import concourse.mybir as mybir
-from concourse.masks import make_identity
 
 K, T, D, V, N = 512, 4096, 3, 512, 128
 S = D * V
@@ -22,13 +21,15 @@ PACK = 4
 PER_COL = 16
 HALF = V // 2
 TAIL = 64
-ORDER = (2, 0, 1, 3)
+PIECES = (0, 1792, 3584, T)
+SCALAR_SHARE = 640
 
 
 def tile_picked_hash_lin_bias_sub_l_kernel(tc, xT, w, b, offs, out):
     nc = tc.nc
     with ExitStack() as ctx:
         keep = ctx.enter_context(tc.tile_pool(name="keep", bufs=1))
+        shared = ctx.enter_context(tc.tile_pool(name="shared", bufs=1))
         psum = ctx.enter_context(tc.psum_pool(name="psum", bufs=1))
 
         offsets = keep.tile([P, S // PER_COL], U16, name="offsets", align_bytes=256)
@@ -36,69 +37,51 @@ def tile_picked_hash_lin_bias_sub_l_kernel(tc, xT, w, b, offs, out):
         w_raw = keep.tile([P, PACK, N], F32, name="w_raw", align_bytes=256)
         bias = keep.tile([P, 1], F32, name="bias")
         x_rows = xT.rearrange("(p t) c -> p t c", t=PACK)
+        last = PACK - 1
 
-        nc.sync.dma_start(planes[ORDER[0]][:], x_rows[:, ORDER[0], :])
+        nc.sync.dma_start(planes[0][:], x_rows[:, 0, :])
         nc.sync.dma_start(offsets[:], offs)
-        for t in ORDER[1:]:
+        for t in range(1, last):
             nc.sync.dma_start(planes[t][:], x_rows[:, t, :])
+        for c0, c1 in zip(PIECES, PIECES[1:]):
+            nc.sync.dma_start(planes[last][:, c0:c1], x_rows[:, last, c0:c1])
         nc.sync.dma_start(w_raw[:], w.rearrange("(p t) m -> p t m", t=PACK))
         nc.sync.dma_start(bias[:], b)
 
-        ident = keep.tile([P, P], F32, name="ident")
-        make_identity(nc, ident[:])
         ones = keep.tile([P, HALF], F32, name="ones")
-        ones_y = keep.tile([P, P], F32, name="ones_y", tag="a", align_bytes=64)
-        ones_z = keep.tile([P, P], F32, name="ones_z", tag="b", align_bytes=64)
-        for filled in (ones, ones_y, ones_z):
-            nc.gpsimd.memset(filled[:], 1.0)
+        nc.vector.memset(ones[:], 1.0)
         x_grouped = keep.tile([P, V, PACK], BF16, name="x_grouped", align_bytes=64)
         x_scales = keep.tile([P, V], U8, name="x_scales", align_bytes=64)
         w_grouped = keep.tile([P, N, PACK], BF16, name="w_grouped", align_bytes=64)
         w_scales = keep.tile([P, N], U8, name="w_scales", align_bytes=64)
         result = keep.tile([P, V], F32, name="result", align_bytes=256)
+        sums_low = keep.tile([P, 2, V], F32, name="sums_low", align_bytes=64)
+        sums_high = [keep.tile([P, 2, HALF], F32, name=f"sums_high{h}", align_bytes=64) for h in range(2)]
 
-        def gather(t, d, cols, before, tag, op=ADD):
-            v0, v1 = cols
-            piece = offsets[:, (d * V + v0) // PER_COL : (d * V + v1) // PER_COL]
-            looked_up = planes[t][:].indirect(piece)
-            total = keep.tile([P, v1 - v0], F32, name="total", tag=tag, align_bytes=64)
-            if before is not None:
-                nc.vector.tensor_tensor(total[:], looked_up, before, op)
-            else:
-                nc.vector.tensor_copy(total[:], looked_up)
-            return total
+        def piece(d, v0, v1):
+            return offsets[:, (d * V + v0) // PER_COL : (d * V + v1) // PER_COL]
 
-        def interleave(t, cols, total):
-            v0, v1 = cols
-            if t == last and v1 == V:
-                nc.scalar.copy(x_grouped[:, v0 : V - TAIL, t], total[:, : V - TAIL - v0])
-                nc.vector.tensor_copy(x_grouped[:, V - TAIL : V, t], total[:, V - TAIL - v0 :])
-            else:
-                nc.scalar.copy(x_grouped[:, v0:v1, t], total[:])
+        def partial(width, tag):
+            return keep.tile([P, width], F32, name="partial", tag=tag, align_bytes=64)
 
-        def sum_on_tensor_engine(t):
-            turned = [psum.tile([P, P], F32, name="turned", bufs=4) for v0 in range(0, V, P)]
-            for d in range(D):
-                picked = gather(t, d, (0, V), None, f"picked{d}")
-                for j, bank in enumerate(turned):
-                    nc.tensor.matmul(
-                        bank[:],
-                        picked[:, j * P : (j + 1) * P],
-                        ident[:],
-                        start=(d == 0),
-                        stop=(d == D - 1),
-                        is_transpose=True,
-                    )
-            staged = keep.tile([P, V], F32, name="staged")
-            for j, bank in enumerate(turned):
-                nc.scalar.copy(staged[:, j * P : (j + 1) * P], bank[:])
-            back = psum.tile([P, V], F32, name="back")
-            for j in range(0, V, P):
-                nc.tensor.transpose(back[:, j : j + P], staged[:, j : j + P], ident[:])
-            if t + 1 == last:
-                nc.scalar.copy(x_grouped[:, :, t : t + 2], back[:].unsqueeze(2).to_broadcast([P, V, 2]))
-            else:
-                nc.scalar.copy(x_grouped[:, :, t], back[:])
+        def gather(total, t, d, v0, v1, before, op=ADD):
+            nc.vector.tensor_tensor(total, planes[t][:].indirect(piece(d, v0, v1)), before, op)
+
+        def early_plane(t, targets):
+            one = partial(V, "one")
+            nc.vector.tensor_copy(one[:], planes[t][:].indirect(piece(0, 0, V)))
+            two = [partial(HALF, f"two{h}") for h in range(2)]
+            for h in range(2):
+                gather(two[h][:], t, 1, h * HALF, (h + 1) * HALF, one[:, h * HALF : (h + 1) * HALF])
+            for h in range(2):
+                gather(targets[h], t, 2, h * HALF, (h + 1) * HALF, two[h][:])
+
+        def high_sum(v0, v1):
+            return sums_high[v0 // HALF][:, 1, v0 % HALF : v0 % HALF + v1 - v0]
+
+        def round_high(copy, v0, v1):
+            both = sums_high[v0 // HALF][:, :, v0 % HALF : v0 % HALF + v1 - v0]
+            copy(x_grouped[:, v0:v1, 2:4], both.rearrange("p t v -> p v t"))
 
         def quantize_x(x_codes, v0, v1):
             nc.vector.quantize_mx(
@@ -123,40 +106,50 @@ def tile_picked_hash_lin_bias_sub_l_kernel(tc, xT, w, b, offs, out):
             else:
                 nc.vector.tensor_scalar(result[:, v0:v1], acc[:], bias[:], None, ADD)
 
-        last = PACK - 1
-        halves = ((0, HALF), (HALF, V))
-        for t in ORDER[:2]:
-            sum_on_tensor_engine(t)
-        for t in ORDER[2:3]:
-            one = gather(t, 0, (0, V), None, "early0")
-            two = [gather(t, 1, h, one[:, h[0] : h[1]], f"early1_{h[0]}") for h in halves]
-            three = [gather(t, 2, h, s[:], f"early2_{h[0]}") for h, s in zip(halves, two)]
-            for h, s in zip(halves, three):
-                interleave(t, h, s)
+        for t in range(2):
+            early_plane(t, [sums_low[:, t, h * HALF : (h + 1) * HALF] for h in range(2)])
+        nc.scalar.copy(x_grouped[:, :, 0:2], sums_low[:].rearrange("p t v -> p v t"))
+        early_plane(2, [sums_high[h][:, 0, :] for h in range(2)])
+
+        narrow = shared.tile([P, T], BF16, name="narrow", offset=0, align_bytes=64)
+        cut = PIECES[1] + SCALAR_SHARE
+        nc.scalar.copy(narrow[:, : PIECES[1]], planes[last][:, : PIECES[1]])
+        nc.scalar.copy(narrow[:, PIECES[1] : cut], planes[last][:, PIECES[1] : cut])
+        nc.vector.tensor_copy(narrow[:, cut : PIECES[2]], planes[last][:, cut : PIECES[2]])
+        nc.scalar.copy(narrow[:, PIECES[2] :], planes[last][:, PIECES[2] :])
 
         nc.scalar.copy(w_grouped[:], w_raw[:].rearrange("p t m -> p m t"))
+        a, bb, c, q = ((v0, v0 + P) for v0 in range(0, V, P))
+        picked = [keep.tile([P, P], BF16, name=f"picked{d}", align_bytes=64) for d in range(2)]
+        for d in range(2):
+            nc.scalar.activation(picked[d][:], narrow[:].indirect(piece(d, *q)), ACT.Copy)
 
-        first, third, fourth = (0, HALF), (HALF, HALF + P), (HALF + P, V)
-        x0 = gather(last, 0, first, ones[:], "x0", MULT)
-        y0 = gather(last, 0, third, ones_y[:], "y0", MULT)
-        x1 = gather(last, 1, first, x0[:], "x1")
-        z0 = gather(last, 0, fourth, ones_z[:], "a", MULT)
-        x2 = gather(last, 2, first, x1[:], "x2")
-        interleave(last, first, x2)
-        y1 = gather(last, 1, third, y0[:], "b")
-        z1 = gather(last, 1, fourth, z0[:], "z1")
-        y2 = gather(last, 2, third, y1[:], "y2")
-        interleave(last, third, y2)
-        z2 = gather(last, 2, fourth, z1[:], "z2")
-        w_codes = keep.tile([P, N], U32, name="w_codes", align_bytes=64)
+        ab0 = partial(HALF, "ab0")
+        c0, a1, b1, q1 = (partial(P, tag) for tag in ("c0", "a1", "b1", "q1"))
+        gather(ab0[:], last, 0, 0, HALF, ones[:], MULT)
+        gather(c0[:], last, 0, *c, ones[:, :P], MULT)
+        gather(a1[:], last, 1, *a, ab0[:, :P])
+        gather(b1[:], last, 1, *bb, ab0[:, P:])
+        gather(high_sum(*a), last, 2, *a, a1[:])
+        round_high(nc.scalar.copy, *a)
+        gather(high_sum(*bb), last, 2, *bb, b1[:])
+        round_high(nc.scalar.copy, *bb)
+        c1 = shared.tile([P, P], F32, name="c1", offset=0, align_bytes=64)
+        gather(c1[:], last, 1, *c, c0[:])
+        nc.vector.tensor_tensor(q1[:], picked[0][:], picked[1][:], ADD)
+        w_codes = shared.tile([P, N], U32, name="w_codes", offset=4 * V, align_bytes=64)
         nc.vector.quantize_mx(
             out=w_codes[:].bitcast(FP8X4), scales=w_scales[:], in_=w_grouped[:].rearrange("p m t -> p (m t)")
         )
-        x_codes = keep.tile([P, V], U32, name="x_codes", tag="b", align_bytes=64)
-        quantize_x(x_codes, *first)
-        interleave(last, fourth, z2)
-        quantize_x(x_codes, *third)
-        quantize_x(x_codes, *fourth)
-        for cols, on_scalar in ((first, True), (third, True), (fourth, False)):
+        gather(high_sum(*c), last, 2, *c, c1[:])
+        round_high(nc.scalar.copy, *c)
+        gather(high_sum(*q), last, 2, *q, q1[:])
+        x_codes = shared.tile([P, V], U32, name="x_codes", offset=0, align_bytes=64)
+        quantize_x(x_codes, 0, HALF)
+        round_high(nc.scalar.copy, q[0], V - TAIL)
+        round_high(nc.vector.tensor_copy, V - TAIL, V)
+        quantize_x(x_codes, *c)
+        quantize_x(x_codes, *q)
+        for cols, on_scalar in (((0, HALF), True), (c, True), (q, False)):
             product(x_codes, w_codes, *cols, on_scalar)
             nc.sync.dma_start(out[:, cols[0] : cols[1]], result[:, cols[0] : cols[1]])

@@ -21,8 +21,8 @@ PACK = 4
 PER_COL = 16
 HALF = V // 2
 TAIL = 64
-PIECES = (0, 1792, 3584, T)
-SCALAR_SHARE = 640
+PIECES = (0, 1536, 2944, 3840, 4096)
+SCALAR_SHARES = (1536, 896, 256, 256)
 
 
 def tile_picked_hash_lin_bias_sub_l_kernel(tc, xT, w, b, offs, out):
@@ -34,7 +34,8 @@ def tile_picked_hash_lin_bias_sub_l_kernel(tc, xT, w, b, offs, out):
 
         offsets = keep.tile([P, S // PER_COL], U16, name="offsets", align_bytes=256)
         planes = [keep.tile([P, T], F32, name=f"plane{t}", align_bytes=256) for t in range(PACK)]
-        w_raw = keep.tile([P, PACK, N], F32, name="w_raw", align_bytes=256)
+        late = keep.tile([P, HALF + P + PACK * N], F32, name="late", align_bytes=256)
+        w_raw = late[:, HALF + P :].rearrange("p (t m) -> p t m", t=PACK)
         bias = keep.tile([P, 1], F32, name="bias")
         x_rows = xT.rearrange("(p t) c -> p t c", t=PACK)
         last = PACK - 1
@@ -45,24 +46,24 @@ def tile_picked_hash_lin_bias_sub_l_kernel(tc, xT, w, b, offs, out):
             nc.sync.dma_start(planes[t][:], x_rows[:, t, :])
         for c0, c1 in zip(PIECES, PIECES[1:]):
             nc.sync.dma_start(planes[last][:, c0:c1], x_rows[:, last, c0:c1])
-        nc.sync.dma_start(w_raw[:], w.rearrange("(p t) m -> p t m", t=PACK))
+        nc.sync.dma_start(w_raw, w.rearrange("(p t) m -> p t m", t=PACK))
         nc.sync.dma_start(bias[:], b)
 
-        ones = keep.tile([P, HALF], F32, name="ones")
+        ones = keep.tile([P, P], F32, name="ones")
         nc.vector.memset(ones[:], 1.0)
         x_grouped = keep.tile([P, V, PACK], BF16, name="x_grouped", align_bytes=64)
         x_scales = keep.tile([P, V], U8, name="x_scales", align_bytes=64)
         w_grouped = keep.tile([P, N, PACK], BF16, name="w_grouped", align_bytes=64)
         w_scales = keep.tile([P, N], U8, name="w_scales", align_bytes=64)
-        result = keep.tile([P, V], F32, name="result", align_bytes=256)
         sums_low = keep.tile([P, 2, V], F32, name="sums_low", align_bytes=64)
-        sums_high = [keep.tile([P, 2, HALF], F32, name=f"sums_high{h}", align_bytes=64) for h in range(2)]
+        early = keep.tile([P, V], F32, name="early", align_bytes=64)
+        sums_high = [both[:, :V].rearrange("p (t v) -> p t v", t=2) for both in (early, late)]
 
         def piece(d, v0, v1):
             return offsets[:, (d * V + v0) // PER_COL : (d * V + v1) // PER_COL]
 
         def partial(width, tag):
-            return keep.tile([P, width], F32, name="partial", tag=tag, align_bytes=64)
+            return keep.tile([P, width], F32, name="partial", tag=tag, align_bytes=256)
 
         def gather(total, t, d, v0, v1, before, op=ADD):
             nc.vector.tensor_tensor(total, planes[t][:].indirect(piece(d, v0, v1)), before, op)
@@ -90,7 +91,7 @@ def tile_picked_hash_lin_bias_sub_l_kernel(tc, xT, w, b, offs, out):
                 in_=x_grouped[:, v0:v1, :].rearrange("p v t -> p (v t)"),
             )
 
-        def product(x_codes, w_codes, v0, v1, on_scalar):
+        def product(result, x_codes, w_codes, v0, v1, on_scalar):
             acc = psum.tile([P, v1 - v0], F32, name=f"acc{v0}")
             nc.tensor.matmul_mx(
                 out=acc[:],
@@ -102,9 +103,9 @@ def tile_picked_hash_lin_bias_sub_l_kernel(tc, xT, w, b, offs, out):
                 stop=True,
             )
             if on_scalar:
-                nc.scalar.activation(result[:, v0:v1], acc[:], ACT.Identity, bias=bias[:])
+                nc.scalar.activation(result[:], acc[:], ACT.Identity, bias=bias[:])
             else:
-                nc.vector.tensor_scalar(result[:, v0:v1], acc[:], bias[:], None, ADD)
+                nc.vector.tensor_scalar(result[:], acc[:], bias[:], None, ADD)
 
         for t in range(2):
             early_plane(t, [sums_low[:, t, h * HALF : (h + 1) * HALF] for h in range(2)])
@@ -112,44 +113,45 @@ def tile_picked_hash_lin_bias_sub_l_kernel(tc, xT, w, b, offs, out):
         early_plane(2, [sums_high[h][:, 0, :] for h in range(2)])
 
         narrow = shared.tile([P, T], BF16, name="narrow", offset=0, align_bytes=64)
-        cut = PIECES[1] + SCALAR_SHARE
-        nc.scalar.copy(narrow[:, : PIECES[1]], planes[last][:, : PIECES[1]])
-        nc.scalar.copy(narrow[:, PIECES[1] : cut], planes[last][:, PIECES[1] : cut])
-        nc.vector.tensor_copy(narrow[:, cut : PIECES[2]], planes[last][:, cut : PIECES[2]])
-        nc.scalar.copy(narrow[:, PIECES[2] :], planes[last][:, PIECES[2] :])
+        for c0, c1, share in zip(PIECES, PIECES[1:], SCALAR_SHARES):
+            nc.scalar.copy(narrow[:, c0 : c0 + share], planes[last][:, c0 : c0 + share])
+            if c0 + share < c1:
+                nc.vector.tensor_copy(narrow[:, c0 + share : c1], planes[last][:, c0 + share : c1])
 
-        nc.scalar.copy(w_grouped[:], w_raw[:].rearrange("p t m -> p m t"))
-        a, bb, c, q = ((v0, v0 + P) for v0 in range(0, V, P))
-        picked = [keep.tile([P, P], BF16, name=f"picked{d}", align_bytes=64) for d in range(2)]
-        for d in range(2):
-            nc.scalar.activation(picked[d][:], narrow[:].indirect(piece(d, *q)), ACT.Copy)
+        a, bb, c, q = [(v0, v0 + P) for v0 in range(0, V, P)]
+        picked = {}
+        for block in (c, q):
+            for d in range(2):
+                picked[block, d] = keep.tile([P, P], BF16, name=f"picked{block[0]}_{d}", align_bytes=64)
+                nc.scalar.activation(picked[block, d][:], narrow[:].indirect(piece(d, *block)), ACT.Copy)
+        nc.scalar.copy(w_grouped[:], w_raw.rearrange("p t m -> p m t"))
 
-        ab0 = partial(HALF, "ab0")
-        c0, a1, b1, q1 = (partial(P, tag) for tag in ("c0", "a1", "b1", "q1"))
-        gather(ab0[:], last, 0, 0, HALF, ones[:], MULT)
-        gather(c0[:], last, 0, *c, ones[:, :P], MULT)
-        gather(a1[:], last, 1, *a, ab0[:, :P])
-        gather(b1[:], last, 1, *bb, ab0[:, P:])
+        a0, b0, a1, b1, c1, q1 = (partial(P, tag) for tag in ("a0", "b0", "a1", "b1", "c1", "q1"))
+        gather(a0[:], last, 0, *a, ones[:], MULT)
+        gather(b0[:], last, 0, *bb, ones[:], MULT)
+        gather(a1[:], last, 1, *a, a0[:])
+        gather(b1[:], last, 1, *bb, b0[:])
         gather(high_sum(*a), last, 2, *a, a1[:])
         round_high(nc.scalar.copy, *a)
         gather(high_sum(*bb), last, 2, *bb, b1[:])
-        round_high(nc.scalar.copy, *bb)
-        c1 = shared.tile([P, P], F32, name="c1", offset=0, align_bytes=64)
-        gather(c1[:], last, 1, *c, c0[:])
-        nc.vector.tensor_tensor(q1[:], picked[0][:], picked[1][:], ADD)
-        w_codes = shared.tile([P, N], U32, name="w_codes", offset=4 * V, align_bytes=64)
+        nc.vector.tensor_tensor(c1[:], picked[c, 0][:], picked[c, 1][:], ADD)
+        round_high(nc.vector.tensor_copy, *bb)
+        gather(high_sum(*c), last, 2, *c, c1[:])
+        round_high(nc.scalar.copy, *c)
+        nc.vector.tensor_tensor(q1[:], picked[q, 0][:], picked[q, 1][:], ADD)
+        w_codes = keep.tile([P, N], U32, name="w_codes", align_bytes=64)
         nc.vector.quantize_mx(
             out=w_codes[:].bitcast(FP8X4), scales=w_scales[:], in_=w_grouped[:].rearrange("p m t -> p (m t)")
         )
-        gather(high_sum(*c), last, 2, *c, c1[:])
-        round_high(nc.scalar.copy, *c)
-        gather(high_sum(*q), last, 2, *q, q1[:])
         x_codes = shared.tile([P, V], U32, name="x_codes", offset=0, align_bytes=64)
-        quantize_x(x_codes, 0, HALF)
+        quantize_x(x_codes, *bb)
+        gather(high_sum(*q), last, 2, *q, q1[:])
+        quantize_x(x_codes, *a)
         round_high(nc.scalar.copy, q[0], V - TAIL)
         round_high(nc.vector.tensor_copy, V - TAIL, V)
         quantize_x(x_codes, *c)
         quantize_x(x_codes, *q)
-        for cols, on_scalar in (((0, HALF), True), (c, True), (q, False)):
-            product(x_codes, w_codes, *cols, on_scalar)
-            nc.sync.dma_start(out[:, cols[0] : cols[1]], result[:, cols[0] : cols[1]])
+        for cols, tag in ((bb, "q1"), (a, "a0"), (c, "b0"), (q, "a1")):
+            result = partial(P, tag)
+            product(result, x_codes, w_codes, *cols, cols != q)
+            nc.sync.dma_start(out[:, cols[0] : cols[1]], result[:])

@@ -21,8 +21,8 @@ PACK = 4
 PER_COL = 16
 HALF = V // 2
 TAIL = 64
-PIECES = (0, 1536, 2944, 3840, 4096)
-SCALAR_SHARES = (1536, 896, 256, 256)
+PIECES = (0, 1408, 2816, 3840, 4096)
+SCALAR_SHARES = (1408, 1408, 128, 256)
 
 
 def tile_picked_hash_lin_bias_sub_l_kernel(tc, xT, w, b, offs, out):
@@ -53,7 +53,7 @@ def tile_picked_hash_lin_bias_sub_l_kernel(tc, xT, w, b, offs, out):
         nc.vector.memset(ones[:], 1.0)
         x_grouped = keep.tile([P, V, PACK], BF16, name="x_grouped", align_bytes=64)
         x_scales = keep.tile([P, V], U8, name="x_scales", align_bytes=64)
-        w_grouped = keep.tile([P, N, PACK], BF16, name="w_grouped", align_bytes=64)
+        w_grouped = keep.tile([P, N, PACK], BF16, name="w_grouped", tag="w_grouped", align_bytes=64)
         w_scales = keep.tile([P, N], U8, name="w_scales", align_bytes=64)
         sums_low = keep.tile([P, 2, V], F32, name="sums_low", align_bytes=64)
         early = keep.tile([P, V], F32, name="early", align_bytes=64)
@@ -133,19 +133,19 @@ def tile_picked_hash_lin_bias_sub_l_kernel(tc, xT, w, b, offs, out):
         gather(b1[:], last, 1, *bb, b0[:])
         gather(high_sum(*a), last, 2, *a, a1[:])
         round_high(nc.scalar.copy, *a)
-        gather(high_sum(*bb), last, 2, *bb, b1[:])
         nc.vector.tensor_tensor(c1[:], picked[c, 0][:], picked[c, 1][:], ADD)
-        round_high(nc.vector.tensor_copy, *bb)
+        gather(high_sum(*bb), last, 2, *bb, b1[:])
         gather(high_sum(*c), last, 2, *c, c1[:])
         round_high(nc.scalar.copy, *c)
         nc.vector.tensor_tensor(q1[:], picked[q, 0][:], picked[q, 1][:], ADD)
+        round_high(nc.vector.tensor_copy, *bb)
         w_codes = keep.tile([P, N], U32, name="w_codes", align_bytes=64)
         nc.vector.quantize_mx(
             out=w_codes[:].bitcast(FP8X4), scales=w_scales[:], in_=w_grouped[:].rearrange("p m t -> p (m t)")
         )
-        x_codes = shared.tile([P, V], U32, name="x_codes", offset=0, align_bytes=64)
-        quantize_x(x_codes, *bb)
         gather(high_sum(*q), last, 2, *q, q1[:])
+        x_codes = keep.tile([P, V], U32, name="x_codes", tag="w_grouped", align_bytes=64)
+        quantize_x(x_codes, *bb)
         quantize_x(x_codes, *a)
         round_high(nc.scalar.copy, q[0], V - TAIL)
         round_high(nc.vector.tensor_copy, V - TAIL, V)

@@ -21,8 +21,8 @@ PACK = 4
 PER_COL = 16
 HALF = V // 2
 TAIL = 64
-PIECES = (0, 1408, 2816, 3840, 4096)
-SCALAR_SHARES = (1408, 1408, 128, 256)
+PIECES = (0, 1536, 3072, 3840, 4096)
+SCALAR_SHARES = (1536, 896, 256, 256)
 
 
 def tile_picked_hash_lin_bias_sub_l_kernel(tc, xT, w, b, offs, out):
@@ -124,7 +124,9 @@ def tile_picked_hash_lin_bias_sub_l_kernel(tc, xT, w, b, offs, out):
             for d in range(2):
                 picked[block, d] = keep.tile([P, P], BF16, name=f"picked{block[0]}_{d}", align_bytes=64)
                 nc.scalar.activation(picked[block, d][:], narrow[:].indirect(piece(d, *block)), ACT.Copy)
-        nc.scalar.copy(w_grouped[:], w_raw.rearrange("p t m -> p m t"))
+        nc.scalar.copy(
+            w_grouped[:].rearrange("p (c i) t -> p c t i", i=4), w_raw.rearrange("p t (c i) -> p c t i", i=4)
+        )
 
         a0, b0, a1, b1, c1, q1 = (partial(P, tag) for tag in ("a0", "b0", "a1", "b1", "c1", "q1"))
         gather(a0[:], last, 0, *a, ones[:], MULT)

@@ -134,26 +134,26 @@ def tile_picked_hash_lin_bias_sub_l_kernel(tc, xT, w, b, offs, out):
         gather(a1[:], last, 1, *a, a0[:])
         gather(b1[:], last, 1, *bb, b0[:])
         gather(high_sum(*a), last, 2, *a, a1[:])
-        round_high(nc.scalar.copy, *a)
-        nc.vector.tensor_tensor(c1[:], picked[c, 0][:], picked[c, 1][:], ADD)
         gather(high_sum(*bb), last, 2, *bb, b1[:])
+        round_high(nc.scalar.copy, *bb)
+        nc.vector.tensor_tensor(c1[:], picked[c, 0][:], picked[c, 1][:], ADD)
+        round_high(nc.vector.tensor_copy, *a)
+        nc.vector.tensor_tensor(q1[:], picked[q, 0][:], picked[q, 1][:], ADD)
         gather(high_sum(*c), last, 2, *c, c1[:])
         round_high(nc.scalar.copy, *c)
-        nc.vector.tensor_tensor(q1[:], picked[q, 0][:], picked[q, 1][:], ADD)
-        round_high(nc.vector.tensor_copy, *bb)
         w_codes = keep.tile([P, N], U32, name="w_codes", align_bytes=64)
         nc.vector.quantize_mx(
             out=w_codes[:].bitcast(FP8X4), scales=w_scales[:], in_=w_grouped[:].rearrange("p m t -> p (m t)")
         )
         gather(high_sum(*q), last, 2, *q, q1[:])
         x_codes = keep.tile([P, V], U32, name="x_codes", tag="w_grouped", align_bytes=64)
-        quantize_x(x_codes, *bb)
         quantize_x(x_codes, *a)
+        quantize_x(x_codes, *bb)
         round_high(nc.scalar.copy, q[0], V - TAIL)
         round_high(nc.vector.tensor_copy, V - TAIL, V)
         quantize_x(x_codes, *c)
         quantize_x(x_codes, *q)
-        for cols, tag in ((bb, "q1"), (a, "a0"), (c, "b0"), (q, "a1")):
+        for cols, tag in ((a, "q1"), (bb, "a0"), (c, "b0"), (q, "a1")):
             result = partial(P, tag)
             product(result, x_codes, w_codes, *cols, cols != q)
             nc.sync.dma_start(out[:, cols[0] : cols[1]], result[:])

@@ -21,15 +21,12 @@ PACK = 4
 PER_COL = 16
 HALF = V // 2
 TAIL = 64
-PIECES = (0, 1536, 3072, 3840, 4096)
-SCALAR_SHARES = (1536, 896, 256, 256)
 
 
 def tile_picked_hash_lin_bias_sub_l_kernel(tc, xT, w, b, offs, out):
     nc = tc.nc
     with ExitStack() as ctx:
         keep = ctx.enter_context(tc.tile_pool(name="keep", bufs=1))
-        shared = ctx.enter_context(tc.tile_pool(name="shared", bufs=1))
         psum = ctx.enter_context(tc.psum_pool(name="psum", bufs=1))
 
         offsets = keep.tile([P, S // PER_COL], U16, name="offsets", align_bytes=256)
@@ -42,10 +39,8 @@ def tile_picked_hash_lin_bias_sub_l_kernel(tc, xT, w, b, offs, out):
 
         nc.sync.dma_start(planes[0][:], x_rows[:, 0, :])
         nc.sync.dma_start(offsets[:], offs)
-        for t in range(1, last):
+        for t in range(1, PACK):
             nc.sync.dma_start(planes[t][:], x_rows[:, t, :])
-        for c0, c1 in zip(PIECES, PIECES[1:]):
-            nc.sync.dma_start(planes[last][:, c0:c1], x_rows[:, last, c0:c1])
         nc.sync.dma_start(w_raw, w.rearrange("(p t) m -> p t m", t=PACK))
         nc.sync.dma_start(bias[:], b)
 
@@ -68,14 +63,19 @@ def tile_picked_hash_lin_bias_sub_l_kernel(tc, xT, w, b, offs, out):
         def gather(total, t, d, v0, v1, before, op=ADD):
             nc.vector.tensor_tensor(total, planes[t][:].indirect(piece(d, v0, v1)), before, op)
 
+        def pick(values, t, d, v0, v1):
+            nc.scalar.activation(values, planes[t][:].indirect(piece(d, v0, v1)), ACT.Copy)
+
         def early_plane(t, targets):
-            one = partial(V, "one")
-            nc.vector.tensor_copy(one[:], planes[t][:].indirect(piece(0, 0, V)))
+            halves = [(h * HALF, (h + 1) * HALF) for h in range(2)]
+            one = [partial(HALF, f"one{h}") for h in range(2)]
             two = [partial(HALF, f"two{h}") for h in range(2)]
             for h in range(2):
-                gather(two[h][:], t, 1, h * HALF, (h + 1) * HALF, one[:, h * HALF : (h + 1) * HALF])
+                pick(one[h][:], t, 0, *halves[h])
             for h in range(2):
-                gather(targets[h], t, 2, h * HALF, (h + 1) * HALF, two[h][:])
+                gather(two[h][:], t, 1, *halves[h], one[h][:])
+            for h in range(2):
+                gather(targets[h], t, 2, *halves[h], two[h][:])
 
         def high_sum(v0, v1):
             return sums_high[v0 // HALF][:, 1, v0 % HALF : v0 % HALF + v1 - v0]
@@ -109,21 +109,15 @@ def tile_picked_hash_lin_bias_sub_l_kernel(tc, xT, w, b, offs, out):
 
         for t in range(2):
             early_plane(t, [sums_low[:, t, h * HALF : (h + 1) * HALF] for h in range(2)])
-        nc.scalar.copy(x_grouped[:, :, 0:2], sums_low[:].rearrange("p t v -> p v t"))
         early_plane(2, [sums_high[h][:, 0, :] for h in range(2)])
-
-        narrow = shared.tile([P, T], BF16, name="narrow", offset=0, align_bytes=64)
-        for c0, c1, share in zip(PIECES, PIECES[1:], SCALAR_SHARES):
-            nc.scalar.copy(narrow[:, c0 : c0 + share], planes[last][:, c0 : c0 + share])
-            if c0 + share < c1:
-                nc.vector.tensor_copy(narrow[:, c0 + share : c1], planes[last][:, c0 + share : c1])
+        nc.scalar.copy(x_grouped[:, :, 0:2], sums_low[:].rearrange("p t v -> p v t"))
 
         a, bb, c, q = [(v0, v0 + P) for v0 in range(0, V, P)]
         picked = {}
         for block in (c, q):
             for d in range(2):
-                picked[block, d] = keep.tile([P, P], BF16, name=f"picked{block[0]}_{d}", align_bytes=64)
-                nc.scalar.activation(picked[block, d][:], narrow[:].indirect(piece(d, *block)), ACT.Copy)
+                picked[block, d] = partial(P, f"picked{block[0]}_{d}")
+                pick(picked[block, d][:], last, d, *block)
         nc.scalar.copy(
             w_grouped[:].rearrange("p (c i) t -> p c t i", i=4), w_raw.rearrange("p t (c i) -> p c t i", i=4)
         )
@@ -135,9 +129,9 @@ def tile_picked_hash_lin_bias_sub_l_kernel(tc, xT, w, b, offs, out):
         gather(b1[:], last, 1, *bb, b0[:])
         gather(high_sum(*a), last, 2, *a, a1[:])
         gather(high_sum(*bb), last, 2, *bb, b1[:])
+        round_high(nc.scalar.copy, *a)
         round_high(nc.scalar.copy, *bb)
         nc.vector.tensor_tensor(c1[:], picked[c, 0][:], picked[c, 1][:], ADD)
-        round_high(nc.vector.tensor_copy, *a)
         nc.vector.tensor_tensor(q1[:], picked[q, 0][:], picked[q, 1][:], ADD)
         gather(high_sum(*c), last, 2, *c, c1[:])
         round_high(nc.scalar.copy, *c)

@@ -46,13 +46,14 @@ def tile_picked_hash_lin_bias_sub_l_kernel(tc, xT, w, b, offs, out):
 
         ones = keep.tile([P, P], F32, name="ones")
         nc.vector.memset(ones[:], 1.0)
-        x_grouped = keep.tile([P, V, PACK], BF16, name="x_grouped", align_bytes=64)
         x_scales = keep.tile([P, V], U8, name="x_scales", align_bytes=64)
         w_grouped = keep.tile([P, N, PACK], BF16, name="w_grouped", tag="w_grouped", align_bytes=64)
         w_scales = keep.tile([P, N], U8, name="w_scales", align_bytes=64)
         sums_low = keep.tile([P, 2, V], F32, name="sums_low", align_bytes=64)
         early = keep.tile([P, V], F32, name="early", align_bytes=64)
         sums_high = [both[:, :V].rearrange("p (t v) -> p t v", t=2) for both in (early, late)]
+
+        blocks = [(v0, v0 + P) for v0 in range(0, V, P)]
 
         def piece(d, v0, v1):
             return offsets[:, (d * V + v0) // PER_COL : (d * V + v1) // PER_COL]
@@ -66,19 +67,19 @@ def tile_picked_hash_lin_bias_sub_l_kernel(tc, xT, w, b, offs, out):
         def pick(values, t, d, v0, v1):
             nc.scalar.activation(values, planes[t][:].indirect(piece(d, v0, v1)), ACT.Copy)
 
-        def early_plane(t, targets):
-            halves = [(h * HALF, (h + 1) * HALF) for h in range(2)]
-            one = [partial(HALF, f"one{h}") for h in range(2)]
-            two = [partial(HALF, f"two{h}") for h in range(2)]
-            for h in range(2):
-                pick(one[h][:], t, 0, *halves[h])
-            for h in range(2):
-                gather(two[h][:], t, 1, *halves[h], one[h][:])
-            for h in range(2):
-                gather(targets[h], t, 2, *halves[h], two[h][:])
+        def early_plane(t, target, first_tag="one0"):
+            one = [partial(P, tag) for tag in (first_tag, "one1", "one2", "one3")]
+            two = [partial(P, f"two{j}") for j in range(len(blocks))]
+            for values, block in zip(one, blocks):
+                pick(values[:], t, 0, *block)
+            for j in range(len(blocks) + 1):
+                if j < len(blocks):
+                    gather(two[j][:], t, 1, *blocks[j], one[j][:])
+                if j > 0:
+                    gather(target(*blocks[j - 1]), t, 2, *blocks[j - 1], two[j - 1][:])
 
-        def high_sum(v0, v1):
-            return sums_high[v0 // HALF][:, 1, v0 % HALF : v0 % HALF + v1 - v0]
+        def high_sum(v0, v1, row=1):
+            return sums_high[v0 // HALF][:, row, v0 % HALF : v0 % HALF + v1 - v0]
 
         def round_high(copy, v0, v1):
             both = sums_high[v0 // HALF][:, :, v0 % HALF : v0 % HALF + v1 - v0]
@@ -108,11 +109,12 @@ def tile_picked_hash_lin_bias_sub_l_kernel(tc, xT, w, b, offs, out):
                 nc.vector.tensor_scalar(result[:], acc[:], bias[:], None, ADD)
 
         for t in range(2):
-            early_plane(t, [sums_low[:, t, h * HALF : (h + 1) * HALF] for h in range(2)])
-        early_plane(2, [sums_high[h][:, 0, :] for h in range(2)])
+            early_plane(t, lambda v0, v1: sums_low[:, t, v0:v1])
+        early_plane(2, lambda v0, v1: high_sum(v0, v1, 0), "x_grouped")
+        x_grouped = keep.tile([P, V, PACK], BF16, name="x_grouped", tag="x_grouped", align_bytes=256)
         nc.scalar.copy(x_grouped[:, :, 0:2], sums_low[:].rearrange("p t v -> p v t"))
 
-        a, bb, c, q = [(v0, v0 + P) for v0 in range(0, V, P)]
+        a, bb, c, q = blocks
         picked = {}
         for block in (c, q):
             for d in range(2):

@@ -67,16 +67,15 @@ def tile_picked_hash_lin_bias_sub_l_kernel(tc, xT, w, b, offs, out):
         def pick(values, t, d, v0, v1):
             nc.scalar.activation(values, planes[t][:].indirect(piece(d, v0, v1)), ACT.Copy)
 
-        def early_plane(t, target, first_tag="one0"):
-            one = [partial(P, tag) for tag in (first_tag, "one1", "one2", "one3")]
-            two = [partial(P, f"two{j}") for j in range(len(blocks))]
-            for values, block in zip(one, blocks):
-                pick(values[:], t, 0, *block)
-            for j in range(len(blocks) + 1):
-                if j < len(blocks):
-                    gather(two[j][:], t, 1, *blocks[j], one[j][:])
-                if j > 0:
-                    gather(target(*blocks[j - 1]), t, 2, *blocks[j - 1], two[j - 1][:])
+        def early_plane(t, target):
+            halves = ((0, HALF), (HALF, V))
+            one = partial(V, "one")
+            nc.vector.tensor_copy(one[:], planes[t][:].indirect(piece(0, 0, V)))
+            two = [partial(HALF, f"two{h}") for h in range(2)]
+            for values, (v0, v1) in zip(two, halves):
+                gather(values[:], t, 1, v0, v1, one[:, v0:v1])
+            for values, (v0, v1) in zip(two, halves):
+                gather(target(v0, v1), t, 2, v0, v1, values[:])
 
         def high_sum(v0, v1, row=1):
             return sums_high[v0 // HALF][:, row, v0 % HALF : v0 % HALF + v1 - v0]
@@ -110,8 +109,8 @@ def tile_picked_hash_lin_bias_sub_l_kernel(tc, xT, w, b, offs, out):
 
         for t in range(2):
             early_plane(t, lambda v0, v1: sums_low[:, t, v0:v1])
-        early_plane(2, lambda v0, v1: high_sum(v0, v1, 0), "x_grouped")
-        x_grouped = keep.tile([P, V, PACK], BF16, name="x_grouped", tag="x_grouped", align_bytes=256)
+        early_plane(2, lambda v0, v1: high_sum(v0, v1, 0))
+        x_grouped = keep.tile([P, V, PACK], BF16, name="x_grouped", align_bytes=64)
         nc.scalar.copy(x_grouped[:, :, 0:2], sums_low[:].rearrange("p t v -> p v t"))
 
         a, bb, c, q = blocks

@@ -103,9 +103,9 @@ def tile_picked_hash_lin_bias_sub_l_kernel(tc, xT, w, b, offs, out):
                 stop=True,
             )
             if on_scalar:
-                nc.scalar.activation(result[:], acc[:], ACT.Identity, bias=bias[:])
+                nc.scalar.activation(result, acc[:], ACT.Identity, bias=bias[:])
             else:
-                nc.vector.tensor_scalar(result[:], acc[:], bias[:], None, ADD)
+                nc.vector.tensor_scalar(result, acc[:], bias[:], None, ADD)
 
         for t in range(2):
             early_plane(t, lambda v0, v1: sums_low[:, t, v0:v1])
@@ -117,7 +117,7 @@ def tile_picked_hash_lin_bias_sub_l_kernel(tc, xT, w, b, offs, out):
         picked = {}
         for block in (c, q):
             for d in range(2):
-                picked[block, d] = partial(P, f"picked{block[0]}_{d}")
+                picked[block, d] = keep.tile([P, P], BF16, name=f"picked{block[0]}_{d}", align_bytes=256)
                 pick(picked[block, d][:], last, d, *block)
         nc.scalar.copy(
             w_grouped[:].rearrange("p (c i) t -> p c t i", i=4), w_raw.rearrange("p t (c i) -> p c t i", i=4)
@@ -144,11 +144,17 @@ def tile_picked_hash_lin_bias_sub_l_kernel(tc, xT, w, b, offs, out):
         x_codes = keep.tile([P, V], U32, name="x_codes", tag="w_grouped", align_bytes=64)
         quantize_x(x_codes, *a)
         quantize_x(x_codes, *bb)
-        round_high(nc.scalar.copy, q[0], V - TAIL)
-        round_high(nc.vector.tensor_copy, V - TAIL, V)
+        ends = ((q[0], V - TAIL), (V - TAIL, V))
+        round_high(nc.vector.tensor_copy, *ends[0])
+        round_high(nc.scalar.copy, *ends[1])
         quantize_x(x_codes, *c)
-        quantize_x(x_codes, *q)
-        for cols, tag in ((a, "q1"), (bb, "a0"), (c, "b0"), (q, "a1")):
+        for cols in ends:
+            quantize_x(x_codes, *cols)
+        for cols, tag in ((a, "q1"), (bb, "a0"), (c, "b0")):
             result = partial(P, tag)
-            product(result, x_codes, w_codes, *cols, cols != q)
+            product(result[:], x_codes, w_codes, *cols, True)
             nc.sync.dma_start(out[:, cols[0] : cols[1]], result[:])
+        result = partial(P, "a1")
+        for v0, v1 in ends:
+            product(result[:, v0 - q[0] : v1 - q[0]], x_codes, w_codes, v0, v1, False)
+        nc.sync.dma_start(out[:, q[0] : q[1]], result[:])

@@ -21,16 +21,22 @@ PACK = 4
 PER_COL = 16
 HALF = V // 2
 TAIL = 64
+KIB = 1024
+PLACES = ((0, 64 * KIB), (16 * KIB, 256), (32 * KIB, 256), (56 * KIB, 256))
 
 
 def tile_picked_hash_lin_bias_sub_l_kernel(tc, xT, w, b, offs, out):
     nc = tc.nc
     with ExitStack() as ctx:
         keep = ctx.enter_context(tc.tile_pool(name="keep", bufs=1))
+        table = ctx.enter_context(tc.tile_pool(name="table", bufs=1))
         psum = ctx.enter_context(tc.psum_pool(name="psum", bufs=1))
 
         offsets = keep.tile([P, S // PER_COL], U16, name="offsets", align_bytes=256)
-        planes = [keep.tile([P, T], F32, name=f"plane{t}", align_bytes=256) for t in range(PACK)]
+        planes = [
+            table.tile([P, T], F32, name=f"plane{t}", offset=start, align_bytes=align)
+            for t, (start, align) in enumerate(PLACES)
+        ]
         late = keep.tile([P, HALF + P + PACK * N], F32, name="late", align_bytes=256)
         w_raw = late[:, HALF + P :].rearrange("p (t m) -> p t m", t=PACK)
         bias = keep.tile([P, 1], F32, name="bias")

@@ -14,15 +14,13 @@ U8 = mybir.dt.uint8
 FP8X4 = mybir.dt.float8_e4m3fn_x4
 ACT = mybir.ActivationFunctionType
 ADD = mybir.AluOpType.add
-MULT = mybir.AluOpType.mult
+AXIS_X = mybir.AxisListType.X
 
 P = 128
 PACK = 4
 PER_COL = 16
 HALF = V // 2
 TAIL = 64
-KIB = 1024
-PLACES = ((0, 64 * KIB), (16 * KIB, 256), (32 * KIB, 256), (56 * KIB, 256))
 
 
 def tile_picked_hash_lin_bias_sub_l_kernel(tc, xT, w, b, offs, out):
@@ -33,12 +31,8 @@ def tile_picked_hash_lin_bias_sub_l_kernel(tc, xT, w, b, offs, out):
         psum = ctx.enter_context(tc.psum_pool(name="psum", bufs=1))
 
         offsets = keep.tile([P, S // PER_COL], U16, name="offsets", align_bytes=256)
-        planes = [
-            table.tile([P, T], F32, name=f"plane{t}", offset=start, align_bytes=align)
-            for t, (start, align) in enumerate(PLACES)
-        ]
-        late = keep.tile([P, HALF + P + PACK * N], F32, name="late", align_bytes=256)
-        w_raw = late[:, HALF + P :].rearrange("p (t m) -> p t m", t=PACK)
+        planes = [table.tile([P, T], F32, name=f"plane{t}", align_bytes=256) for t in range(PACK)]
+        w_raw = keep.tile([P, PACK, N], F32, name="w_raw", align_bytes=256)
         bias = keep.tile([P, 1], F32, name="bias")
         x_rows = xT.rearrange("(p t) c -> p t c", t=PACK)
         last = PACK - 1
@@ -47,19 +41,19 @@ def tile_picked_hash_lin_bias_sub_l_kernel(tc, xT, w, b, offs, out):
         nc.sync.dma_start(offsets[:], offs)
         for t in range(1, PACK):
             nc.sync.dma_start(planes[t][:], x_rows[:, t, :])
-        nc.sync.dma_start(w_raw, w.rearrange("(p t) m -> p t m", t=PACK))
+        nc.sync.dma_start(w_raw[:], w.rearrange("(p t) m -> p t m", t=PACK))
         nc.sync.dma_start(bias[:], b)
 
-        ones = keep.tile([P, P], F32, name="ones")
-        nc.vector.memset(ones[:], 1.0)
+        x_grouped = keep.tile([P, V, PACK], BF16, name="x_grouped", align_bytes=64)
+        x_codes = keep.tile([P, V], U32, name="x_codes", align_bytes=64)
         x_scales = keep.tile([P, V], U8, name="x_scales", align_bytes=64)
-        w_grouped = keep.tile([P, N, PACK], BF16, name="w_grouped", tag="w_grouped", align_bytes=64)
+        w_grouped = keep.tile([P, N, PACK], BF16, name="w_grouped", align_bytes=64)
+        w_codes = keep.tile([P, N], U32, name="w_codes", align_bytes=64)
         w_scales = keep.tile([P, N], U8, name="w_scales", align_bytes=64)
         sums_low = keep.tile([P, 2, V], F32, name="sums_low", align_bytes=64)
-        early = keep.tile([P, V], F32, name="early", align_bytes=64)
-        sums_high = [both[:, :V].rearrange("p (t v) -> p t v", t=2) for both in (early, late)]
-
-        blocks = [(v0, v0 + P) for v0 in range(0, V, P)]
+        third = keep.tile([P, HALF], F32, name="third", align_bytes=64)
+        sums_high = keep.tile([P, 2, HALF], F32, name="sums_high", align_bytes=64)
+        result = keep.tile([P, V], F32, name="result", align_bytes=256)
 
         def piece(d, v0, v1):
             return offsets[:, (d * V + v0) // PER_COL : (d * V + v1) // PER_COL]
@@ -67,37 +61,34 @@ def tile_picked_hash_lin_bias_sub_l_kernel(tc, xT, w, b, offs, out):
         def partial(width, tag):
             return keep.tile([P, width], F32, name="partial", tag=tag, align_bytes=256)
 
-        def gather(total, t, d, v0, v1, before, op=ADD):
-            nc.vector.tensor_tensor(total, planes[t][:].indirect(piece(d, v0, v1)), before, op)
+        def gather(total, t, d, v0, v1, before):
+            nc.vector.tensor_tensor(total, planes[t][:].indirect(piece(d, v0, v1)), before, ADD)
 
         def pick(values, t, d, v0, v1):
             nc.scalar.activation(values, planes[t][:].indirect(piece(d, v0, v1)), ACT.Copy)
 
-        def early_plane(t, target):
+        def early_plane(t, targets):
             halves = ((0, HALF), (HALF, V))
             one = partial(V, "one")
             nc.vector.tensor_copy(one[:], planes[t][:].indirect(piece(0, 0, V)))
             two = [partial(HALF, f"two{h}") for h in range(2)]
             for values, (v0, v1) in zip(two, halves):
                 gather(values[:], t, 1, v0, v1, one[:, v0:v1])
-            for values, (v0, v1) in zip(two, halves):
-                gather(target(v0, v1), t, 2, v0, v1, values[:])
+            for values, target, (v0, v1) in zip(two, targets, halves):
+                gather(target, t, 2, v0, v1, values[:])
 
-        def high_sum(v0, v1, row=1):
-            return sums_high[v0 // HALF][:, row, v0 % HALF : v0 % HALF + v1 - v0]
+        def round_high(v0, v1):
+            both = sums_high[:, :, v0 - HALF : v1 - HALF]
+            nc.scalar.copy(x_grouped[:, v0:v1, 2:4], both.rearrange("p t v -> p v t"))
 
-        def round_high(copy, v0, v1):
-            both = sums_high[v0 // HALF][:, :, v0 % HALF : v0 % HALF + v1 - v0]
-            copy(x_grouped[:, v0:v1, 2:4], both.rearrange("p t v -> p v t"))
-
-        def quantize_x(x_codes, v0, v1):
+        def quantize_x(v0, v1):
             nc.vector.quantize_mx(
                 out=x_codes[:, v0:v1].bitcast(FP8X4),
                 scales=x_scales[:, v0:v1],
                 in_=x_grouped[:, v0:v1, :].rearrange("p v t -> p (v t)"),
             )
 
-        def product(result, x_codes, w_codes, v0, v1, on_scalar):
+        def product(v0, v1, on_scalar):
             acc = psum.tile([P, v1 - v0], F32, name=f"acc{v0}")
             nc.tensor.matmul_mx(
                 out=acc[:],
@@ -109,58 +100,54 @@ def tile_picked_hash_lin_bias_sub_l_kernel(tc, xT, w, b, offs, out):
                 stop=True,
             )
             if on_scalar:
-                nc.scalar.activation(result, acc[:], ACT.Identity, bias=bias[:])
+                nc.scalar.activation(result[:, v0:v1], acc[:], ACT.Identity, bias=bias[:])
             else:
-                nc.vector.tensor_scalar(result, acc[:], bias[:], None, ADD)
+                nc.vector.tensor_scalar(result[:, v0:v1], acc[:], bias[:], None, ADD)
 
         for t in range(2):
-            early_plane(t, lambda v0, v1: sums_low[:, t, v0:v1])
-        early_plane(2, lambda v0, v1: high_sum(v0, v1, 0))
-        x_grouped = keep.tile([P, V, PACK], BF16, name="x_grouped", align_bytes=64)
+            early_plane(t, (sums_low[:, t, :HALF], sums_low[:, t, HALF:]))
         nc.scalar.copy(x_grouped[:, :, 0:2], sums_low[:].rearrange("p t v -> p v t"))
+        early_plane(2, (third[:], sums_high[:, 0, :]))
+        nc.scalar.copy(x_grouped[:, :HALF, 2], third[:])
 
-        a, bb, c, q = blocks
-        picked = {}
-        for block in (c, q):
-            for d in range(2):
-                picked[block, d] = keep.tile([P, P], BF16, name=f"picked{block[0]}_{d}", align_bytes=256)
-                pick(picked[block, d][:], last, d, *block)
+        c, q, a, bb = [(v0, v0 + P) for v0 in range(0, V, P)]
+        picked = keep.tile([P, D, HALF], BF16, name="picked", align_bytes=256)
+        a0, b0, a1, b1 = (partial(P, tag) for tag in ("a0", "b0", "a1", "b1"))
+
+        def reduce_block(v0, v1):
+            with nc.allow_low_precision(reason="the sum is float32 inside the engine, rounded once on the way out"):
+                nc.vector.tensor_reduce(
+                    x_grouped[:, v0:v1, last], picked[:, :, v0:v1].rearrange("p d v -> p v d"), AXIS_X, ADD
+                )
+
+        nc.vector.tensor_copy(picked[:, 2, :], planes[last][:].indirect(piece(2, 0, HALF)))
+        pick(a0[:], last, 0, *a)
+        pick(b0[:], last, 0, *bb)
+        pick(picked[:, 0, :], last, 0, 0, HALF)
+        for v0, v1 in (c, q):
+            pick(picked[:, 1, v0:v1], last, 1, v0, v1)
         nc.scalar.copy(
-            w_grouped[:].rearrange("p (c i) t -> p c t i", i=4), w_raw.rearrange("p t (c i) -> p c t i", i=4)
+            w_grouped[:].rearrange("p (c i) t -> p c t i", i=4), w_raw[:].rearrange("p t (c i) -> p c t i", i=4)
         )
-
-        a0, b0, a1, b1, c1, q1 = (partial(P, tag) for tag in ("a0", "b0", "a1", "b1", "c1", "q1"))
-        gather(a0[:], last, 0, *a, ones[:], MULT)
-        gather(b0[:], last, 0, *bb, ones[:], MULT)
         gather(a1[:], last, 1, *a, a0[:])
         gather(b1[:], last, 1, *bb, b0[:])
-        gather(high_sum(*a), last, 2, *a, a1[:])
-        gather(high_sum(*bb), last, 2, *bb, b1[:])
-        round_high(nc.scalar.copy, *a)
-        round_high(nc.scalar.copy, *bb)
-        nc.vector.tensor_tensor(c1[:], picked[c, 0][:], picked[c, 1][:], ADD)
-        nc.vector.tensor_tensor(q1[:], picked[q, 0][:], picked[q, 1][:], ADD)
-        gather(high_sum(*c), last, 2, *c, c1[:])
-        round_high(nc.scalar.copy, *c)
-        w_codes = keep.tile([P, N], U32, name="w_codes", align_bytes=64)
+        gather(sums_high[:, 1, a[0] - HALF : a[1] - HALF], last, 2, *a, a1[:])
+        gather(sums_high[:, 1, bb[0] - HALF : bb[1] - HALF], last, 2, *bb, b1[:])
+        ends = ((bb[0], bb[1] - TAIL), (bb[1] - TAIL, bb[1]))
+        round_high(*a)
+        for cols in ends:
+            round_high(*cols)
+        reduce_block(*c)
+        reduce_block(*q)
         nc.vector.quantize_mx(
             out=w_codes[:].bitcast(FP8X4), scales=w_scales[:], in_=w_grouped[:].rearrange("p m t -> p (m t)")
         )
-        gather(high_sum(*q), last, 2, *q, q1[:])
-        x_codes = keep.tile([P, V], U32, name="x_codes", tag="w_grouped", align_bytes=64)
-        quantize_x(x_codes, *a)
-        quantize_x(x_codes, *bb)
-        ends = ((q[0], V - TAIL), (V - TAIL, V))
-        round_high(nc.vector.tensor_copy, *ends[0])
-        round_high(nc.scalar.copy, *ends[1])
-        quantize_x(x_codes, *c)
+        for cols in (c, q, a) + ends:
+            quantize_x(*cols)
+        for cols in (c, q):
+            product(*cols, True)
+            nc.sync.dma_start(out[:, cols[0] : cols[1]], result[:, cols[0] : cols[1]])
+        product(*a, True)
         for cols in ends:
-            quantize_x(x_codes, *cols)
-        for cols, tag in ((a, "q1"), (bb, "a0"), (c, "b0")):
-            result = partial(P, tag)
-            product(result[:], x_codes, w_codes, *cols, True)
-            nc.sync.dma_start(out[:, cols[0] : cols[1]], result[:])
-        result = partial(P, "a1")
-        for v0, v1 in ends:
-            product(result[:, v0 - q[0] : v1 - q[0]], x_codes, w_codes, v0, v1, False)
-        nc.sync.dma_start(out[:, q[0] : q[1]], result[:])
+            product(*cols, False)
+        nc.sync.dma_start(out[:, HALF:], result[:, HALF:])

@@ -14,6 +14,7 @@ U8 = mybir.dt.uint8
 FP8X4 = mybir.dt.float8_e4m3fn_x4
 ACT = mybir.ActivationFunctionType
 ADD = mybir.AluOpType.add
+MULT = mybir.AluOpType.mult
 AXIS_X = mybir.AxisListType.X
 
 P = 128
@@ -44,12 +45,12 @@ def tile_picked_hash_lin_bias_sub_l_kernel(tc, xT, w, b, offs, out):
         nc.sync.dma_start(w_raw[:], w.rearrange("(p t) m -> p t m", t=PACK))
         nc.sync.dma_start(bias[:], b)
 
-        x_grouped = keep.tile([P, V, PACK], BF16, name="x_grouped", align_bytes=64)
-        x_codes = keep.tile([P, V], U32, name="x_codes", align_bytes=64)
-        x_scales = keep.tile([P, V], U8, name="x_scales", align_bytes=64)
-        w_grouped = keep.tile([P, N, PACK], BF16, name="w_grouped", align_bytes=64)
-        w_codes = keep.tile([P, N], U32, name="w_codes", align_bytes=64)
-        w_scales = keep.tile([P, N], U8, name="w_scales", align_bytes=64)
+        grouped = keep.tile([P, N + V, PACK], BF16, name="grouped", align_bytes=64)
+        codes = keep.tile([P, N + V], U32, name="codes", align_bytes=64)
+        scales = keep.tile([P, N + V], U8, name="scales", align_bytes=64)
+        w_grouped, x_grouped = grouped[:, :N, :], grouped[:, N:, :]
+        w_codes, x_codes = codes[:, :N], codes[:, N:]
+        w_scales, x_scales = scales[:, :N], scales[:, N:]
         sums_low = keep.tile([P, 2, V], F32, name="sums_low", align_bytes=64)
         third = keep.tile([P, HALF], F32, name="third", align_bytes=64)
         sums_high = keep.tile([P, 2, HALF], F32, name="sums_high", align_bytes=64)
@@ -92,8 +93,8 @@ def tile_picked_hash_lin_bias_sub_l_kernel(tc, xT, w, b, offs, out):
             acc = psum.tile([P, v1 - v0], F32, name=f"acc{v0}")
             nc.tensor.matmul_mx(
                 out=acc[:],
-                lhsT=w_codes[:].bitcast(FP8X4),
-                lhsT_scale=w_scales[:],
+                lhsT=w_codes.bitcast(FP8X4),
+                lhsT_scale=w_scales,
                 rhs=x_codes[:, v0:v1].bitcast(FP8X4),
                 rhs_scale=x_scales[:, v0:v1],
                 start=True,
@@ -127,27 +128,28 @@ def tile_picked_hash_lin_bias_sub_l_kernel(tc, xT, w, b, offs, out):
         for v0, v1 in (c, q):
             pick(picked[:, 1, v0:v1], last, 1, v0, v1)
         nc.scalar.copy(
-            w_grouped[:].rearrange("p (c i) t -> p c t i", i=4), w_raw[:].rearrange("p t (c i) -> p c t i", i=4)
+            w_grouped.rearrange("p (c i) t -> p c t i", i=4), w_raw[:].rearrange("p t (c i) -> p c t i", i=4)
         )
         gather(a1[:], last, 1, *a, a0[:])
         gather(b1[:], last, 1, *bb, b0[:])
         gather(sums_high[:, 1, a[0] - HALF : a[1] - HALF], last, 2, *a, a1[:])
         gather(sums_high[:, 1, bb[0] - HALF : bb[1] - HALF], last, 2, *bb, b1[:])
-        ends = ((bb[0], bb[1] - TAIL), (bb[1] - TAIL, bb[1]))
-        round_high(*a)
-        for cols in ends:
-            round_high(*cols)
+        nc.gpsimd.tensor_scalar(
+            x_grouped[:, a[0] : a[1], 2:4], sums_high[:, :, :P].rearrange("p t v -> p v t"), 1.0, 0.0, MULT, ADD
+        )
+        round_high(*bb)
         reduce_block(*c)
         reduce_block(*q)
         nc.vector.quantize_mx(
-            out=w_codes[:].bitcast(FP8X4), scales=w_scales[:], in_=w_grouped[:].rearrange("p m t -> p (m t)")
+            out=codes[:, : N + P].bitcast(FP8X4),
+            scales=scales[:, : N + P],
+            in_=grouped[:, : N + P, :].rearrange("p m t -> p (m t)"),
         )
-        for cols in (c, q, a) + ends:
+        for cols in (q, a, bb):
             quantize_x(*cols)
         for cols in (c, q):
             product(*cols, True)
             nc.sync.dma_start(out[:, cols[0] : cols[1]], result[:, cols[0] : cols[1]])
         product(*a, True)
-        for cols in ends:
-            product(*cols, False)
+        product(*bb, False)
         nc.sync.dma_start(out[:, HALF:], result[:, HALF:])

@@ -45,7 +45,7 @@ def tile_picked_hash_lin_bias_sub_l_kernel(tc, xT, w, b, offs, out):
         nc.sync.dma_start(w_raw[:], w.rearrange("(p t) m -> p t m", t=PACK))
         nc.sync.dma_start(bias[:], b)
 
-        grouped = keep.tile([P, N + V, PACK], BF16, name="grouped", align_bytes=64)
+        grouped = keep.tile([P, N + V, PACK], BF16, name="grouped", align_bytes=256)
         codes = keep.tile([P, N + V], U32, name="codes", align_bytes=64)
         scales = keep.tile([P, N + V], U8, name="scales", align_bytes=64)
         w_grouped, x_grouped = grouped[:, :N, :], grouped[:, N:, :]
@@ -113,7 +113,11 @@ def tile_picked_hash_lin_bias_sub_l_kernel(tc, xT, w, b, offs, out):
 
         c, q, a, bb = [(v0, v0 + P) for v0 in range(0, V, P)]
         picked = keep.tile([P, D, HALF], BF16, name="picked", align_bytes=256)
-        a0, b0, a1, b1 = (partial(P, tag) for tag in ("a0", "b0", "a1", "b1"))
+        a0, b0, b1 = (partial(P, tag) for tag in ("a0", "b0", "b1"))
+        a1 = grouped[:, : N // 2, :].rearrange("p m t -> p (m t)").bitcast(F32)
+        w_to = w_grouped.rearrange("p (c i) t -> p c t i", i=4)
+        w_from = w_raw[:].rearrange("p t (c i) -> p c t i", i=4)
+        shared = N // 2 // 4
 
         def reduce_block(v0, v1):
             with nc.allow_low_precision(reason="the sum is float32 inside the engine, rounded once on the way out"):
@@ -127,16 +131,15 @@ def tile_picked_hash_lin_bias_sub_l_kernel(tc, xT, w, b, offs, out):
         pick(picked[:, 0, :], last, 0, 0, HALF)
         for v0, v1 in (c, q):
             pick(picked[:, 1, v0:v1], last, 1, v0, v1)
-        nc.scalar.copy(
-            w_grouped.rearrange("p (c i) t -> p c t i", i=4), w_raw[:].rearrange("p t (c i) -> p c t i", i=4)
-        )
-        gather(a1[:], last, 1, *a, a0[:])
+        nc.scalar.copy(w_to[:, shared:], w_from[:, shared:])
+        gather(a1, last, 1, *a, a0[:])
         gather(b1[:], last, 1, *bb, b0[:])
-        gather(sums_high[:, 1, a[0] - HALF : a[1] - HALF], last, 2, *a, a1[:])
+        gather(sums_high[:, 1, a[0] - HALF : a[1] - HALF], last, 2, *a, a1)
         gather(sums_high[:, 1, bb[0] - HALF : bb[1] - HALF], last, 2, *bb, b1[:])
         nc.gpsimd.tensor_scalar(
-            x_grouped[:, a[0] : a[1], 2:4], sums_high[:, :, :P].rearrange("p t v -> p v t"), 1.0, 0.0, MULT, ADD
+            w_grouped[:, : N // 2, :], w_raw[:, :, : N // 2].rearrange("p t m -> p m t"), 1.0, 0.0, MULT, ADD
         )
+        round_high(*a)
         round_high(*bb)
         reduce_block(*c)
         reduce_block(*q)

@@ -62,8 +62,8 @@ def tile_picked_hash_lin_bias_sub_l_kernel(tc, xT, w, b, offs, out):
         def partial(width, tag):
             return keep.tile([P, width], F32, name="partial", tag=tag, align_bytes=256)
 
-        def gather(total, t, d, v0, v1, before):
-            nc.vector.tensor_tensor(total, planes[t][:].indirect(piece(d, v0, v1)), before, ADD)
+        def gather(total, t, d, v0, v1, before, op=ADD):
+            nc.vector.tensor_tensor(total, planes[t][:].indirect(piece(d, v0, v1)), before, op)
 
         def pick(values, t, d, v0, v1):
             nc.scalar.activation(values, planes[t][:].indirect(piece(d, v0, v1)), ACT.Copy)
@@ -113,6 +113,8 @@ def tile_picked_hash_lin_bias_sub_l_kernel(tc, xT, w, b, offs, out):
 
         c, q, a, bb = [(v0, v0 + P) for v0 in range(0, V, P)]
         picked = keep.tile([P, D, HALF], BF16, name="picked", align_bytes=256)
+        ones = keep.tile([P, P], F32, name="ones")
+        nc.vector.memset(ones[:], 1.0)
         a0, b0, b1 = (partial(P, tag) for tag in ("a0", "b0", "b1"))
         a1 = grouped[:, : N // 2, :].rearrange("p m t -> p (m t)").bitcast(F32)
         w_to = w_grouped.rearrange("p (c i) t -> p c t i", i=4)
@@ -125,12 +127,12 @@ def tile_picked_hash_lin_bias_sub_l_kernel(tc, xT, w, b, offs, out):
                     x_grouped[:, v0:v1, last], picked[:, :, v0:v1].rearrange("p d v -> p v d"), AXIS_X, ADD
                 )
 
-        nc.vector.tensor_copy(picked[:, 2, :], planes[last][:].indirect(piece(2, 0, HALF)))
-        pick(a0[:], last, 0, *a)
-        pick(b0[:], last, 0, *bb)
-        pick(picked[:, 0, :], last, 0, 0, HALF)
+        gather(a0[:], last, 0, *a, ones[:], MULT)
+        gather(b0[:], last, 0, *bb, ones[:], MULT)
+        for d in range(2):
+            pick(picked[:, d, :], last, d, 0, HALF)
         for v0, v1 in (c, q):
-            pick(picked[:, 1, v0:v1], last, 1, v0, v1)
+            pick(picked[:, 2, v0:v1], last, 2, v0, v1)
         nc.scalar.copy(w_to[:, shared:], w_from[:, shared:])
         gather(a1, last, 1, *a, a0[:])
         gather(b1[:], last, 1, *bb, b0[:])
@@ -141,6 +143,7 @@ def tile_picked_hash_lin_bias_sub_l_kernel(tc, xT, w, b, offs, out):
         )
         round_high(*a)
         round_high(*bb)
+        ends = ((bb[0], bb[1] - TAIL), (bb[1] - TAIL, bb[1]))
         reduce_block(*c)
         reduce_block(*q)
         nc.vector.quantize_mx(
@@ -148,11 +151,12 @@ def tile_picked_hash_lin_bias_sub_l_kernel(tc, xT, w, b, offs, out):
             scales=scales[:, : N + P],
             in_=grouped[:, : N + P, :].rearrange("p m t -> p (m t)"),
         )
-        for cols in (q, a, bb):
+        for cols in (q, a) + ends:
             quantize_x(*cols)
         for cols in (c, q):
             product(*cols, True)
             nc.sync.dma_start(out[:, cols[0] : cols[1]], result[:, cols[0] : cols[1]])
         product(*a, True)
-        product(*bb, False)
+        for cols in ends:
+            product(*cols, False)
         nc.sync.dma_start(out[:, HALF:], result[:, HALF:])

@@ -43,7 +43,7 @@ def tile_picked_hash_lin_bias_sub_l_kernel(tc, xT, w, b, offs, out):
         for t in range(1, PACK):
             nc.sync.dma_start(planes[t][:], x_rows[:, t, :])
         nc.sync.dma_start(w_raw[:], w.rearrange("(p t) m -> p t m", t=PACK))
-        nc.sync.dma_start(bias[:], b)
+        nc.gpsimd.dma_start(bias[:], b)
 
         grouped = keep.tile([P, N + V, PACK], BF16, name="grouped", align_bytes=256)
         codes = keep.tile([P, N + V], U32, name="codes", align_bytes=64)
@@ -155,7 +155,7 @@ def tile_picked_hash_lin_bias_sub_l_kernel(tc, xT, w, b, offs, out):
             quantize_x(*cols)
         for cols in (c, q):
             product(*cols, True)
-            nc.sync.dma_start(out[:, cols[0] : cols[1]], result[:, cols[0] : cols[1]])
+        nc.sync.dma_start(out[:, :HALF], result[:, :HALF])
         product(*a, True)
         for cols in ends:
             product(*cols, False)

@@ -156,7 +156,7 @@ def tile_picked_hash_lin_bias_sub_l_kernel(tc, xT, w, b, offs, out):
         for cols in (c, q):
             product(*cols, True)
         nc.sync.dma_start(out[:, :HALF], result[:, :HALF])
-        product(*a, True)
+        product(*a, False)
         for cols in ends:
             product(*cols, False)
         nc.sync.dma_start(out[:, HALF:], result[:, HALF:])

@@ -34,7 +34,7 @@ def tile_picked_hash_lin_bias_sub_l_kernel(tc, xT, w, b, offs, out):
         offsets = keep.tile([P, S // PER_COL], U16, name="offsets", align_bytes=256)
         planes = [table.tile([P, T], F32, name=f"plane{t}", align_bytes=256) for t in range(PACK)]
         w_raw = keep.tile([P, PACK, N], F32, name="w_raw", align_bytes=256)
-        bias = keep.tile([P, 1], F32, name="bias")
+        bias_rows = keep.tile([P, 32], F32, name="bias_rows", align_bytes=64)
         x_rows = xT.rearrange("(p t) c -> p t c", t=PACK)
         last = PACK - 1
 
@@ -43,7 +43,8 @@ def tile_picked_hash_lin_bias_sub_l_kernel(tc, xT, w, b, offs, out):
         for t in range(1, PACK):
             nc.sync.dma_start(planes[t][:], x_rows[:, t, :])
         nc.sync.dma_start(w_raw[:], w.rearrange("(p t) m -> p t m", t=PACK))
-        nc.gpsimd.dma_start(bias[:], b)
+        nc.vector.memset(bias_rows[:], 0.0)
+        nc.gpsimd.dma_start(bias_rows[0:P:32, :], b.rearrange("(q j) o -> q (j o)", j=32))
 
         grouped = keep.tile([P, N + V, PACK], BF16, name="grouped", align_bytes=256)
         codes = keep.tile([P, N + V], U32, name="codes", align_bytes=64)
@@ -101,15 +102,18 @@ def tile_picked_hash_lin_bias_sub_l_kernel(tc, xT, w, b, offs, out):
                 stop=True,
             )
             if on_scalar:
-                nc.scalar.activation(result[:, v0:v1], acc[:], ACT.Identity, bias=bias[:])
+                nc.scalar.activation(result[:, v0:v1], acc[:], ACT.Identity, bias=bias)
             else:
-                nc.vector.tensor_scalar(result[:, v0:v1], acc[:], bias[:], None, ADD)
+                nc.vector.tensor_scalar(result[:, v0:v1], acc[:], bias, None, ADD)
 
         for t in range(2):
             early_plane(t, (sums_low[:, t, :HALF], sums_low[:, t, HALF:]))
         nc.scalar.copy(x_grouped[:, :, 0:2], sums_low[:].rearrange("p t v -> p v t"))
         early_plane(2, (third[:], sums_high[:, 0, :]))
         nc.scalar.copy(x_grouped[:, :HALF, 2], third[:])
+        turned = partial(32, "two0")
+        nc.vector.transpose(turned[:], bias_rows[:])
+        bias = turned[:, 0:1]
 
         c, q, a, bb = [(v0, v0 + P) for v0 in range(0, V, P)]
         picked = keep.tile([P, D, HALF], BF16, name="picked", align_bytes=256)

from contextlib import ExitStack

import concourse.mybir as mybir

K, T, D, V, N = 512, 4096, 3, 512, 128
S = D * V
FLOPS = 2 * K * V * N

F32 = mybir.dt.float32
BF16 = mybir.dt.bfloat16
U32 = mybir.dt.uint32
U16 = mybir.dt.uint16
U8 = mybir.dt.uint8
FP8X4 = mybir.dt.float8_e4m3fn_x4
ACT = mybir.ActivationFunctionType
ADD = mybir.AluOpType.add
MULT = mybir.AluOpType.mult
AXIS_X = mybir.AxisListType.X

P = 128
PACK = 4
PER_COL = 16
HALF = V // 2
TAIL = 64


def tile_picked_hash_lin_bias_sub_l_kernel(tc, xT, w, b, offs, out):
    nc = tc.nc
    with ExitStack() as ctx:
        keep = ctx.enter_context(tc.tile_pool(name="keep", bufs=1))
        table = ctx.enter_context(tc.tile_pool(name="table", bufs=1))
        psum = ctx.enter_context(tc.psum_pool(name="psum", bufs=1))

        offsets = keep.tile([P, S // PER_COL], U16, name="offsets", align_bytes=256)
        planes = [table.tile([P, T], F32, name=f"plane{t}", align_bytes=256) for t in range(PACK)]
        w_raw = keep.tile([P, PACK, N], F32, name="w_raw", align_bytes=256)
        bias_rows = keep.tile([P, 32], F32, name="bias_rows", align_bytes=64)
        x_rows = xT.rearrange("(p t) c -> p t c", t=PACK)
        last = PACK - 1

        nc.sync.dma_start(planes[0][:], x_rows[:, 0, :])
        nc.sync.dma_start(offsets[:], offs)
        for t in range(1, PACK):
            nc.sync.dma_start(planes[t][:], x_rows[:, t, :])
        nc.sync.dma_start(w_raw[:], w.rearrange("(p t) m -> p t m", t=PACK))
        nc.vector.memset(bias_rows[:], 0.0)
        nc.gpsimd.dma_start(bias_rows[0:P:32, :], b.rearrange("(q j) o -> q (j o)", j=32))

        grouped = keep.tile([P, N + V, PACK], BF16, name="grouped", align_bytes=256)
        codes = keep.tile([P, N + V], U32, name="codes", align_bytes=64)
        scales = keep.tile([P, N + V], U8, name="scales", align_bytes=64)
        w_grouped, x_grouped = grouped[:, :N, :], grouped[:, N:, :]
        w_codes, x_codes = codes[:, :N], codes[:, N:]
        w_scales, x_scales = scales[:, :N], scales[:, N:]
        sums_low = keep.tile([P, 2, V], F32, name="sums_low", align_bytes=64)
        third = keep.tile([P, HALF], F32, name="third", align_bytes=64)
        sums_high = keep.tile([P, 2, HALF], F32, name="sums_high", align_bytes=64)
        result = keep.tile([P, V], F32, name="result", align_bytes=256)

        def piece(d, v0, v1):
            return offsets[:, (d * V + v0) // PER_COL : (d * V + v1) // PER_COL]

        def partial(width, tag):
            return keep.tile([P, width], F32, name="partial", tag=tag, align_bytes=256)

        def gather(total, t, d, v0, v1, before, op=ADD):
            nc.vector.tensor_tensor(total, planes[t][:].indirect(piece(d, v0, v1)), before, op)

        def pick(values, t, d, v0, v1):
            nc.scalar.activation(values, planes[t][:].indirect(piece(d, v0, v1)), ACT.Copy)

        def early_plane(t, targets):
            halves = ((0, HALF), (HALF, V))
            one = partial(V, "one")
            nc.vector.tensor_copy(one[:], planes[t][:].indirect(piece(0, 0, V)))
            two = [partial(HALF, f"two{h}") for h in range(2)]
            for values, (v0, v1) in zip(two, halves):
                gather(values[:], t, 1, v0, v1, one[:, v0:v1])
            for values, target, (v0, v1) in zip(two, targets, halves):
                gather(target, t, 2, v0, v1, values[:])

        def round_high(v0, v1):
            both = sums_high[:, :, v0 - HALF : v1 - HALF]
            nc.scalar.copy(x_grouped[:, v0:v1, 2:4], both.rearrange("p t v -> p v t"))

        def quantize_x(v0, v1):
            nc.vector.quantize_mx(
                out=x_codes[:, v0:v1].bitcast(FP8X4),
                scales=x_scales[:, v0:v1],
                in_=x_grouped[:, v0:v1, :].rearrange("p v t -> p (v t)"),
            )

        def product(v0, v1, on_scalar):
            acc = psum.tile([P, v1 - v0], F32, name=f"acc{v0}")
            nc.tensor.matmul_mx(
                out=acc[:],
                lhsT=w_codes.bitcast(FP8X4),
                lhsT_scale=w_scales,
                rhs=x_codes[:, v0:v1].bitcast(FP8X4),
                rhs_scale=x_scales[:, v0:v1],
                start=True,
                stop=True,
            )
            if on_scalar:
                nc.scalar.activation(result[:, v0:v1], acc[:], ACT.Identity, bias=bias)
            else:
                nc.vector.tensor_scalar(result[:, v0:v1], acc[:], bias, None, ADD)

        for t in range(2):
            early_plane(t, (sums_low[:, t, :HALF], sums_low[:, t, HALF:]))
        nc.scalar.copy(x_grouped[:, :, 0:2], sums_low[:].rearrange("p t v -> p v t"))
        early_plane(2, (third[:], sums_high[:, 0, :]))
        nc.scalar.copy(x_grouped[:, :HALF, 2], third[:])
        turned = partial(32, "two0")
        nc.vector.transpose(turned[:], bias_rows[:])
        bias = turned[:, 0:1]

        c, q, a, bb = [(v0, v0 + P) for v0 in range(0, V, P)]
        picked = keep.tile([P, D, HALF], BF16, name="picked", align_bytes=256)
        ones = keep.tile([P, P], F32, name="ones")
        nc.vector.memset(ones[:], 1.0)
        a0, b0, b1 = (partial(P, tag) for tag in ("a0", "b0", "b1"))
        a1 = grouped[:, : N // 2, :].rearrange("p m t -> p (m t)").bitcast(F32)
        w_to = w_grouped.rearrange("p (c i) t -> p c t i", i=4)
        w_from = w_raw[:].rearrange("p t (c i) -> p c t i", i=4)
        shared = N // 2 // 4

        def reduce_block(v0, v1):
            with nc.allow_low_precision(reason="the sum is float32 inside the engine, rounded once on the way out"):
                nc.vector.tensor_reduce(
                    x_grouped[:, v0:v1, last], picked[:, :, v0:v1].rearrange("p d v -> p v d"), AXIS_X, ADD
                )

        gather(a0[:], last, 0, *a, ones[:], MULT)
        gather(b0[:], last, 0, *bb, ones[:], MULT)
        for d in range(2):
            pick(picked[:, d, :], last, d, 0, HALF)
        for v0, v1 in (c, q):
            pick(picked[:, 2, v0:v1], last, 2, v0, v1)
        nc.scalar.copy(w_to[:, shared:], w_from[:, shared:])
        gather(a1, last, 1, *a, a0[:])
        gather(b1[:], last, 1, *bb, b0[:])
        gather(sums_high[:, 1, a[0] - HALF : a[1] - HALF], last, 2, *a, a1)
        gather(sums_high[:, 1, bb[0] - HALF : bb[1] - HALF], last, 2, *bb, b1[:])
        nc.gpsimd.tensor_scalar(
            w_grouped[:, : N // 2, :], w_raw[:, :, : N // 2].rearrange("p t m -> p m t"), 1.0, 0.0, MULT, ADD
        )
        round_high(*a)
        round_high(*bb)
        ends = ((bb[0], bb[1] - TAIL), (bb[1] - TAIL, bb[1]))
        reduce_block(*c)
        reduce_block(*q)
        nc.vector.quantize_mx(
            out=codes[:, : N + P].bitcast(FP8X4),
            scales=scales[:, : N + P],
            in_=grouped[:, : N + P, :].rearrange("p m t -> p (m t)"),
        )
        for cols in (q, a) + ends:
            quantize_x(*cols)
        for cols in (c, q):
            product(*cols, True)
        nc.sync.dma_start(out[:, :HALF], result[:, :HALF])
        product(*a, False)
        for cols in ends:
            product(*cols, False)
        nc.sync.dma_start(out[:, HALF:], result[:, HALF:])
